import numpy as np
import ml_dtypes


def mxq(x, axis, fmt="e4m3"):
    dtype, down = {"e4m3": (ml_dtypes.float8_e4m3fn, 7), "e5m2": (ml_dtypes.float8_e5m2, 14)}[fmt]
    v = np.moveaxis(np.asarray(x, np.float32).astype(ml_dtypes.bfloat16).astype(np.float64), axis, -1)
    blocks = v.reshape(v.shape[:-1] + (-1, 32))
    amax = np.abs(blocks).max(-1, keepdims=True)
    byte = np.maximum(np.where(amax > 0, np.frexp(amax)[1] - 1 + 127, 0) - down, 1)
    scale = np.exp2(byte - 127.0)
    codes = (blocks / scale).astype(np.float32).astype(dtype).astype(np.float64)
    return np.moveaxis((codes * scale).reshape(v.shape), -1, axis)


WIDE = False


def mx_kscale(k):
    if not WIDE:
        return np.ones(k)
    levels = np.array([10, -10, 5, -5, 0])
    if k % 512:
        return np.exp2(np.random.permutation(np.resize(levels, k // 32))).repeat(32)
    a = np.empty((k // 512, 16))
    for p in range(k // 512):
        a[p, :8] = np.random.permutation(np.resize(levels, 8))
        for g in range(8):
            far = levels[np.abs(levels - a[p, g]) >= 10]
            a[p, g + 8] = far[np.random.randint(len(far))]
    return np.exp2(a.ravel()).repeat(32)


def f64(x):
    return np.asarray(x).astype(np.float64)


def striped(idx):
    return np.tile(idx.reshape(-1, 16).T, (8, 1)).astype(np.uint16)


def unstriped(offs):
    return offs[:16].T.reshape(-1).astype(np.int64)


E2M1 = np.array([0.0, 0.5, 1.0, 1.5, 2.0, 3.0, 4.0, 6.0, -0.0, -0.5, -1.0, -1.5, -2.0, -3.0, -4.0, -6.0])


def pack_weight(w, fmt):
    k, n = w.shape
    w = f64(np.asarray(w, np.float32).astype(ml_dtypes.bfloat16)).reshape(k // 32, 32, n)
    amax = np.abs(w).max(1)
    if fmt == "e4m3":
        byte = np.frexp(amax)[1] - 1 + 127 - 7
    else:
        mant, ex = np.frexp(amax / 6.0)
        byte = np.where(mant > 0.5, ex, ex - 1) + 127
    byte = np.clip(np.where(amax > 0, byte, 1), 1, 254)
    scaled = (w * np.exp2(127.0 - byte)[:, None, :]).reshape(k, n).astype(np.float32)
    by_word = np.ascontiguousarray(scaled.reshape(k // 512, 128, 4, n).transpose(0, 1, 3, 2))
    if fmt == "e4m3":
        words = by_word.astype(ml_dtypes.float8_e4m3fn).view(np.uint8)
    else:
        c = by_word.astype(ml_dtypes.float4_e2m1fn).view(np.uint8) & 0xF
        words = (c[..., 0::2] | (c[..., 1::2] << 4)).reshape(k // 512, 128, 2 * n)
    return np.ascontiguousarray(words), np.ascontiguousarray(byte.astype(np.uint8).reshape(k // 512, 16, n))


def unpack_weight(words, scales, fmt):
    g, _, n = scales.shape
    words = np.ascontiguousarray(words).reshape(g, 128, n, -1)
    if fmt == "e4m3":
        vals = words.view(ml_dtypes.float8_e4m3fn).astype(np.float64)
    else:
        nib = np.empty((g, 128, n, 4), np.uint8)
        nib[..., 0::2] = words & 0xF
        nib[..., 1::2] = words >> 4
        vals = E2M1[nib]
    vals = vals * np.repeat(np.exp2(scales.astype(np.float64) - 127.0), 8, axis=1)[..., None]
    return vals.transpose(0, 1, 3, 2).reshape(g * 512, n)


def gelu(v):
    return 0.5 * v * (1.0 + np.tanh(np.sqrt(2.0 / np.pi) * (v + 0.044715 * v**3)))


K, H, N, T, S, A, B, C = 1024, 512, 512, 4096, 2048, 1024, 512, 256

def setup_inputs():
    n = np.random.standard_normal
    s = mx_kscale(K)[:, None]
    u = mx_kscale(H)[:, None]
    tab_words, tab_scales = pack_weight(n((K, T)) * s, "e4m3")
    w1 = (n((K, H)) / np.sqrt(K) / s * u.T).astype(np.float32)
    w2_words, w2_scales = pack_weight(1.5 * n((K, H)) / np.sqrt(K) / s, "e2m1")
    w3 = (0.34 * n((H, N)) / np.sqrt(H) / u**2).astype(np.float32)
    w4_words, w4_scales = pack_weight(0.32 * n((H, N)) / np.sqrt(H) / u, "e4m3")
    w5_words, w5_scales = pack_weight(n((H, N)) / np.sqrt(H) / u**2, "e2m1")
    return {"tab_words": tab_words, "tab_scales": tab_scales, "w1": w1,
            "w2_words": w2_words, "w2_scales": w2_scales, "w3": w3,
            "w4_words": w4_words, "w4_scales": w4_scales,
            "w5_words": w5_words, "w5_scales": w5_scales,
            "offs": striped(np.random.permutation(T)[:S]),
            "pos1": striped(np.random.permutation(S)[:A]), "pos2": striped(np.random.permutation(S)[:A]),
            "pos3": striped(np.random.permutation(A)[:B]), "pos4": striped(np.random.permutation(A)[:B]),
            "pos5": striped(np.random.permutation(B)[:C]), "pos6": striped(np.random.permutation(B)[:C])}

def reference(tab_words, tab_scales, w1, w2_words, w2_scales, w3, w4_words, w4_scales,
              w5_words, w5_scales, offs, pos1, pos2, pos3, pos4, pos5, pos6):
    v = unpack_weight(tab_words, tab_scales, "e4m3")[:, unstriped(offs)]
    mark = mxq(f64(w1), 0, "e4m3").T @ v
    bend = unpack_weight(w2_words, w2_scales, "e2m1").T @ v
    h = mark * np.tanh(bend)
    a1 = h[:, unstriped(pos1)] + h[:, unstriped(pos2)]
    a2 = np.maximum(a1[:, unstriped(pos3)], a1[:, unstriped(pos4)])
    b = a2[:, unstriped(pos5)]
    a3 = b * a2[:, unstriped(pos6)]
    a3q = mxq(a3, 0, "e4m3")
    bq = mxq(b, 0, "e4m3")
    y = mxq(f64(w3), 0, "e4m3").T @ a3q + unpack_weight(w4_words, w4_scales, "e4m3").T @ bq
    jury = unpack_weight(w5_words, w5_scales, "e2m1").T @ a3q
    return np.sin(y) * jury

@@ -1,0 +1,291 @@
+import math
+from contextlib import ExitStack
+
+import concourse.mybir as mybir
+
+K, H, N, T, S, A, B, C = 1024, 512, 512, 4096, 2048, 1024, 512, 256
+FLOPS = 4697620480
+
+F32 = mybir.dt.float32
+BF16 = mybir.dt.bfloat16
+I32 = mybir.dt.int32
+U32 = mybir.dt.uint32
+U16 = mybir.dt.uint16
+U8 = mybir.dt.uint8
+E4M3 = mybir.dt.float8_e4m3fn_x4
+E2M1 = mybir.dt.float4_e2m1fn_x4
+ALU = mybir.AluOpType
+ACT = mybir.ActivationFunctionType
+
+P = 128
+PACK = 4
+PASSES = K // (P * PACK)
+CHUNK = 512
+CHUNKS = S // CHUNK
+LIST_ROWS = 16
+ROUNDER = 1.5 * 2.0**23
+
+
+def tile_list_bricklaying_jury_scores_kernel(
+    tc, tab_words, tab_scales, w1, w2_words, w2_scales, w3, w4_words, w4_scales,
+    w5_words, w5_scales, offs, pos1, pos2, pos3, pos4, pos5, pos6, out,
+):
+    nc = tc.nc
+    with ExitStack() as ctx:
+        lists = ctx.enter_context(tc.tile_pool(name="lists", bufs=1))
+        keep = ctx.enter_context(tc.tile_pool(name="keep", bufs=1))
+        ring = ctx.enter_context(tc.tile_pool(name="ring", bufs=4))
+        psum = ctx.enter_context(tc.psum_pool(name="psum", bufs=1))
+
+        def load_list(name, src):
+            tile = lists.tile([P, src.shape[1]], U16, name=name)
+            nc.sync.dma_start(tile[:], src)
+            return tile
+
+        def entries(tile, first, count):
+            return tile[:, first // LIST_ROWS : (first + count) // LIST_ROWS]
+
+        def load_scale_rows(queue, plane, src):
+            for q in range(4):
+                queue.dma_start(
+                    plane[32 * q : 32 * q + 4].bitcast(I32),
+                    src[:, 4 * q : 4 * q + 4, :].rearrange("a r n -> r a n").bitcast(I32),
+                )
+
+        idx = load_list("idx", offs)
+        tab_sc = keep.tile([P, T], U8, name="tab_sc", tag="tab_sc", align_bytes=64)
+        nc.sync.dma_start(tab_sc[0:32, :].bitcast(I32), tab_scales.rearrange("a q t -> (a q) t").bitcast(I32))
+        nc.vector.memset(tab_sc[32:64, :].bitcast(I32), 0)
+        nc.vector.memset(tab_sc[64:128, :].bitcast(I32), 0)
+
+        w2_sc_raw = keep.tile([P, PASSES, H], U8, name="w2_sc_raw", align_bytes=64)
+        nc.gpsimd.memset(w2_sc_raw[:].rearrange("p a n -> p (a n)").bitcast(I32), 0)
+        load_scale_rows(nc.scalar, w2_sc_raw, w2_scales)
+        v_sc = [keep.tile([P, S], U8, name=f"v_sc{a}", align_bytes=64) for a in range(PASSES)]
+        for a in range(PASSES):
+            nc.gpsimd.memset(v_sc[a][:].bitcast(I32), 0)
+        w4_sc = keep.tile([P, 1, N], U8, name="w4_sc", align_bytes=64)
+        w5_sc = keep.tile([P, 1, N], U8, name="w5_sc", align_bytes=64)
+        nc.gpsimd.memset(w4_sc[:, 0, :].bitcast(I32), 0)
+        nc.gpsimd.memset(w5_sc[:, 0, :].bitcast(I32), 0)
+
+        tab_w = [keep.tile([P, T], U32, name=f"tab_w{a}", tag=f"tab_w{a}", align_bytes=64) for a in range(PASSES)]
+        w1_raw = [keep.tile([P, PACK, H], F32, name=f"w1_raw{a}") for a in range(PASSES)]
+        w2_raw = keep.tile([P, PASSES, 2 * H], U8, name="w2_raw", align_bytes=64)
+
+        def load_table(a):
+            nc.sync.dma_start(tab_w[a][:].bitcast(I32), tab_words[a].rearrange("p t i -> p (t i)").bitcast(I32))
+
+        def load_w1(a):
+            nc.sync.dma_start(w1_raw[a][:], w1[a * 512 : (a + 1) * 512, :].rearrange("(p j) n -> p j n", j=PACK))
+
+        load_table(0)
+        nc.sync.dma_start(w2_raw[:].bitcast(I32), w2_words.rearrange("a p b -> p a b").bitcast(I32))
+        load_w1(0)
+        load_table(1)
+        load_w1(1)
+        p1 = load_list("p1", pos1)
+        p2 = load_list("p2", pos2)
+        p3 = load_list("p3", pos3)
+        p4 = load_list("p4", pos4)
+        p5 = load_list("p5", pos5)
+        p6 = load_list("p6", pos6)
+        w3_raw = keep.tile([P, PACK, N], F32, name="w3_raw")
+        nc.sync.dma_start(w3_raw[:], w3.rearrange("(p j) n -> p j n", j=PACK))
+        w4_c = keep.tile([P, N], U32, name="w4_c", align_bytes=64)
+        nc.sync.dma_start(w4_c[:].bitcast(I32), w4_words[0].rearrange("p n i -> p (n i)").bitcast(I32))
+        w5_c = keep.tile([P, 2 * N], U8, name="w5_c", align_bytes=64)
+        nc.sync.dma_start(w5_c[:].bitcast(I32), w5_words[0].bitcast(I32))
+        load_scale_rows(nc.sync, w4_sc, w4_scales)
+        load_scale_rows(nc.sync, w5_sc, w5_scales)
+
+        picked_sc = keep.tile([P, S], U8, name="picked_sc", align_bytes=64)
+        nc.vector.tensor_copy(picked_sc[:], tab_sc[:].indirect(idx[:]))
+        for a in range(PASSES):
+            for q in range(4):
+                row = 16 * a + 4 * q
+                nc.gpsimd.dma_start(v_sc[a][32 * q : 32 * q + 4, :].bitcast(I32), picked_sc[row : row + 4, :].bitcast(I32))
+
+        v0 = keep.tile([P, S], U32, name="v0", align_bytes=64)
+        nc.vector.tensor_copy(v0[:], tab_w[0][:].indirect(idx[:]))
+
+        w2_c = keep.tile([P, PASSES, PACK, 2 * P], U8, name="w2_c", tag="tab_w0", align_bytes=64)
+        w2_sc = keep.tile([P, PASSES, PACK, P], U8, name="w2_sc", tag="tab_sc", align_bytes=64)
+        nc.vector.tensor_copy(
+            w2_c[:].bitcast(U16), w2_raw[:].bitcast(U16).rearrange("p a (m t) -> p a t m", t=PACK)
+        )
+        nc.vector.tensor_copy(w2_sc[:], w2_sc_raw[:].rearrange("p a (m t) -> p a t m", t=PACK))
+
+        w1_c = [keep.tile([P, H], U32, name=f"w1_c{a}", align_bytes=64) for a in range(PASSES)]
+        w1_sc = [keep.tile([P, H], U8, name=f"w1_sc{a}", align_bytes=64) for a in range(PASSES)]
+
+        def quantise_w1(a, t0, t1):
+            n = t1 - t0
+            woven = keep.tile([P, n * P * PACK], BF16, name=f"w1_bf{a}_{t0}", tag=f"w1_bf{a}_{t0}", align_bytes=64)
+            nc.scalar.copy(
+                woven[:].rearrange("p (t m j) -> p m t j", t=n, j=PACK),
+                w1_raw[a][:].rearrange("p j (m t) -> p m t j", t=PACK)[:, :, t0:t1, :],
+            )
+            nc.vector.quantize_mx(
+                out=w1_c[a][:, t0 * P : t1 * P].bitcast(E4M3), scales=w1_sc[a][:, t0 * P : t1 * P], in_=woven[:]
+            )
+
+        quantise_w1(0, 0, 4)
+
+        v1 = []
+        for c in range(CHUNKS):
+            if c == CHUNKS - 1:
+                quantise_w1(1, 0, 1)
+            tag = "w1_bf1_0" if c == CHUNKS - 1 else f"v1_{c}"
+            words = keep.tile([P, CHUNK], U32, name=f"v1_{c}", tag=tag, align_bytes=64)
+            nc.vector.tensor_copy(words[:], tab_w[1][:].indirect(entries(idx, c * CHUNK, CHUNK)))
+            v1.append(words)
+        quantise_w1(1, 1, 4)
+
+        def v_codes(a, c):
+            words = v0[:, c * CHUNK : (c + 1) * CHUNK] if a == 0 else v1[c][:]
+            return words.bitcast(E4M3)
+
+        def mark_pass(bank, t, c, a):
+            cols = slice(t * P, (t + 1) * P)
+            nc.tensor.matmul_mx(
+                out=bank[:], lhsT=w1_c[a][:, cols].bitcast(E4M3), lhsT_scale=w1_sc[a][:, cols],
+                rhs=v_codes(a, c), rhs_scale=v_sc[a][:, c * CHUNK : (c + 1) * CHUNK],
+                start=(a == 0), stop=(a == PASSES - 1),
+            )
+
+        def bend_pass(bank, t, c, a):
+            nc.tensor.matmul_mx(
+                out=bank[:], lhsT=w2_c[:, a, t, :].bitcast(E2M1), lhsT_scale=w2_sc[:, a, t, :],
+                rhs=v_codes(a, c), rhs_scale=v_sc[a][:, c * CHUNK : (c + 1) * CHUNK],
+                start=(a == 0), stop=(a == PASSES - 1),
+            )
+
+        h = [keep.tile([P, S], F32, name=f"h{t}") for t in range(PACK)]
+        a1 = [keep.tile([P, A], F32, name=f"a1_{t}") for t in range(PACK)]
+        a2 = [keep.tile([P, B], F32, name=f"a2_{t}") for t in range(PACK)]
+        b4 = keep.tile([P, PACK, C], F32, name="b4")
+        a34 = keep.tile([P, PACK, C], F32, name="a34")
+
+        def first_stage(t):
+            marks = [psum.tile([P, CHUNK], F32, name=f"mark{c}", tag=f"mark{c}") for c in range(CHUNKS)]
+            bends = [psum.tile([P, CHUNK], F32, name=f"bend{c}", tag=f"bend{c}") for c in range(CHUNKS)]
+            if t == 0:
+                order = [(c, a) for a in range(PASSES) for c in range(CHUNKS)]
+            else:
+                order = [(c, a) for c in range(CHUNKS) for a in range(PASSES)]
+            for c, a in order:
+                bend_pass(bends[c], t, c, a)
+                mark_pass(marks[c], t, c, a)
+                if a == PASSES - 1:
+                    th = ring.tile([P, CHUNK], F32, name="th")
+                    nc.scalar.activation(th[:], bends[c][:], ACT.Tanh)
+                    nc.vector.tensor_tensor(h[t][:, c * CHUNK : (c + 1) * CHUNK], marks[c][:], th[:], ALU.mult)
+
+        def level_one(t):
+            half = A // 2
+            firsts = []
+            for u in range(2):
+                first = ring.tile([P, half], F32, name="first")
+                nc.vector.tensor_copy(first[:], h[t][:].indirect(entries(p1, u * half, half)))
+                firsts.append(first)
+            for u in range(2):
+                nc.vector.tensor_tensor(
+                    a1[t][:, u * half : (u + 1) * half], h[t][:].indirect(entries(p2, u * half, half)), firsts[u][:], ALU.add
+                )
+
+        walls = {}
+
+        def level_two_pick(t):
+            left = ring.tile([P, B], F32, name="left")
+            right = ring.tile([P, B], F32, name="right")
+            nc.vector.tensor_copy(left[:], a1[t][:].indirect(p3[:]))
+            nc.vector.tensor_copy(right[:], a1[t][:].indirect(p4[:]))
+            walls[t] = (left, right)
+
+        def level_two_max(t):
+            left, right = walls[t]
+            nc.vector.tensor_tensor(a2[t][:], left[:], right[:], ALU.max)
+
+        first_stage(0)
+        for t in range(PACK):
+            level_one(t)
+            if t + 1 < PACK:
+                first_stage(t + 1)
+            if t > 0:
+                level_two_max(t - 1)
+            level_two_pick(t)
+            if t == 1:
+                w3_bf = keep.tile([P, N * PACK], BF16, name="w3_bf", align_bytes=64)
+                nc.scalar.copy(
+                    w3_bf[:].rearrange("p (c i j) -> p c j i", i=4, j=PACK),
+                    w3_raw[:].rearrange("p j (c i) -> p c j i", i=4),
+                )
+                w3_c = keep.tile([P, N], U32, name="w3_c", align_bytes=64)
+                w3_sc = keep.tile([P, N], U8, name="w3_sc", align_bytes=64)
+                nc.vector.quantize_mx(out=w3_c[:].bitcast(E4M3), scales=w3_sc[:], in_=w3_bf[:])
+
+        for t in range(PACK):
+            if t == PACK - 1:
+                level_two_max(t)
+            nc.vector.tensor_copy(b4[:, t, :], a2[t][:].indirect(p5[:]))
+        b_bf = keep.tile([P, C * PACK], BF16, name="b_bf", align_bytes=64)
+        nc.scalar.copy(
+            b_bf[:].rearrange("p (c i t) -> p c t i", i=4, t=PACK), b4[:].rearrange("p t (c i) -> p c t i", i=4)
+        )
+        for t in range(PACK):
+            nc.vector.tensor_tensor(a34[:, t, :], a2[t][:].indirect(p6[:]), b4[:, t, :], ALU.mult)
+        b_c = keep.tile([P, C], U32, name="b_c", align_bytes=64)
+        b_sc = keep.tile([P, C], U8, name="b_sc", align_bytes=64)
+        a3_bf = keep.tile([P, C * PACK], BF16, name="a3_bf", align_bytes=64)
+        nc.vector.tensor_copy(
+            a3_bf[:].rearrange("p (c i t) -> p c t i", i=4, t=PACK), a34[:].rearrange("p t (c i) -> p c t i", i=4)
+        )
+        nc.vector.quantize_mx(out=b_c[:].bitcast(E4M3), scales=b_sc[:], in_=b_bf[:])
+        a3_c = keep.tile([P, C], U32, name="a3_c", align_bytes=64)
+        a3_sc = keep.tile([P, C], U8, name="a3_sc", align_bytes=64)
+        nc.vector.quantize_mx(out=a3_c[:].bitcast(E4M3), scales=a3_sc[:], in_=a3_bf[:])
+
+        tiles = N // P
+        ys = [psum.tile([P, C], F32, name=f"y{m}", tag=f"mark{m}") for m in range(tiles)]
+        juries = [psum.tile([P, C], F32, name=f"jury{m}", tag=f"bend{m}") for m in range(tiles)]
+        for m in range(tiles):
+            cols = slice(m * P, (m + 1) * P)
+            nc.tensor.matmul_mx(
+                out=ys[m][:], lhsT=w4_c[:, cols].bitcast(E4M3), lhsT_scale=w4_sc[:, 0, cols],
+                rhs=b_c[:].bitcast(E4M3), rhs_scale=b_sc[:], start=True, stop=False,
+            )
+        for m in range(tiles):
+            cols = slice(m * P, (m + 1) * P)
+            nc.tensor.matmul_mx(
+                out=ys[m][:], lhsT=w3_c[:, cols].bitcast(E4M3), lhsT_scale=w3_sc[:, cols],
+                rhs=a3_c[:].bitcast(E4M3), rhs_scale=a3_sc[:], start=False, stop=True,
+            )
+        for m in range(tiles):
+            nc.tensor.matmul_mx(
+                out=juries[m][:], lhsT=w5_c[:, 2 * m * P : 2 * (m + 1) * P].bitcast(E2M1),
+                lhsT_scale=w5_sc[:, 0, m * P : (m + 1) * P],
+                rhs=a3_c[:].bitcast(E4M3), rhs_scale=a3_sc[:], start=True, stop=True,
+            )
+        turns, wholes, fracs, sines = [], [], [], []
+        for m in range(tiles):
+            turn = ring.tile([P, C], F32, name="turn")
+            nc.scalar.activation(turn[:], ys[m][:], ACT.Copy, scale=1.0 / (2.0 * math.pi))
+            turns.append(turn)
+        for m in range(tiles):
+            whole = ring.tile([P, C], I32, name="whole")
+            nc.vector.tensor_scalar(whole[:], turns[m][:], ROUNDER, ROUNDER, ALU.add, ALU.subtract)
+            wholes.append(whole)
+            if m > 0:
+                frac = ring.tile([P, C], F32, name="frac")
+                nc.vector.tensor_tensor(frac[:], turns[m - 1][:], wholes[m - 1][:], ALU.subtract)
+                fracs.append(frac)
+        frac = ring.tile([P, C], F32, name="frac")
+        nc.vector.tensor_tensor(frac[:], turns[tiles - 1][:], wholes[tiles - 1][:], ALU.subtract)
+        fracs.append(frac)
+        for m in range(tiles):
+            sine = ring.tile([P, C], F32, name="sine")
+            nc.scalar.activation(sine[:], fracs[m][:], ACT.Sin, scale=2.0 * math.pi)
+            score = ring.tile([P, C], F32, name="score")
+            nc.vector.tensor_tensor(score[:], juries[m][:], sine[:], ALU.mult)
+            nc.sync.dma_start(out[m * P : (m + 1) * P, :], score[:])

@@ -23,6 +23,7 @@ PASSES = K // (P * PACK)
 CHUNK = 512
 CHUNKS = S // CHUNK
 LIST_ROWS = 16
+VECTOR_GATES = 6
 ROUNDER = 1.5 * 2.0**23
 
 
@@ -54,20 +55,16 @@ def tile_list_bricklaying_jury_scores_kernel(
 
         idx = load_list("idx", offs)
         tab_sc = keep.tile([P, T], U8, name="tab_sc", tag="tab_sc", align_bytes=64)
-        nc.sync.dma_start(tab_sc[0:32, :].bitcast(I32), tab_scales.rearrange("a q t -> (a q) t").bitcast(I32))
-        nc.vector.memset(tab_sc[32:64, :].bitcast(I32), 0)
-        nc.vector.memset(tab_sc[64:128, :].bitcast(I32), 0)
-
-        w2_sc_raw = keep.tile([P, PASSES, H], U8, name="w2_sc_raw", align_bytes=64)
-        nc.gpsimd.memset(w2_sc_raw[:].rearrange("p a n -> p (a n)").bitcast(I32), 0)
+        nc.sync.dma_start(tab_sc[96:128, :].bitcast(I32), tab_scales.rearrange("a q t -> (a q) t").bitcast(I32))
+        w_sc = keep.tile([P, PASSES + 2, H], U8, name="w_sc", align_bytes=64)
+        nc.vector.memset(w_sc[:].rearrange("p a n -> p (a n)").bitcast(I32), 0)
+        nc.vector.memset(tab_sc[0:96, :].bitcast(I32), 0)
+        v_sc = keep.tile([P, PASSES, S], U8, name="v_sc", align_bytes=64)
+        nc.vector.memset(v_sc[:].rearrange("p a n -> p (a n)").bitcast(I32), 0)
+        w2_sc_raw = w_sc[:, 0:PASSES, :]
+        w4_sc = w_sc[:, PASSES : PASSES + 1, :]
+        w5_sc = w_sc[:, PASSES + 1 : PASSES + 2, :]
         load_scale_rows(nc.scalar, w2_sc_raw, w2_scales)
-        v_sc = [keep.tile([P, S], U8, name=f"v_sc{a}", align_bytes=64) for a in range(PASSES)]
-        for a in range(PASSES):
-            nc.gpsimd.memset(v_sc[a][:].bitcast(I32), 0)
-        w4_sc = keep.tile([P, 1, N], U8, name="w4_sc", align_bytes=64)
-        w5_sc = keep.tile([P, 1, N], U8, name="w5_sc", align_bytes=64)
-        nc.gpsimd.memset(w4_sc[:, 0, :].bitcast(I32), 0)
-        nc.gpsimd.memset(w5_sc[:, 0, :].bitcast(I32), 0)
 
         tab_w = [keep.tile([P, T], U32, name=f"tab_w{a}", tag=f"tab_w{a}", align_bytes=64) for a in range(PASSES)]
         w1_raw = [keep.tile([P, PACK, H], F32, name=f"w1_raw{a}") for a in range(PASSES)]
@@ -103,8 +100,8 @@ def tile_list_bricklaying_jury_scores_kernel(
         nc.vector.tensor_copy(picked_sc[:], tab_sc[:].indirect(idx[:]))
         for a in range(PASSES):
             for q in range(4):
-                row = 16 * a + 4 * q
-                nc.gpsimd.dma_start(v_sc[a][32 * q : 32 * q + 4, :].bitcast(I32), picked_sc[row : row + 4, :].bitcast(I32))
+                row = 96 + 16 * a + 4 * q
+                nc.gpsimd.dma_start(v_sc[32 * q : 32 * q + 4, a, :].bitcast(I32), picked_sc[row : row + 4, :].bitcast(I32))
 
         v0 = keep.tile([P, S], U32, name="v0", align_bytes=64)
         nc.vector.tensor_copy(v0[:], tab_w[0][:].indirect(idx[:]))
@@ -114,18 +111,19 @@ def tile_list_bricklaying_jury_scores_kernel(
         nc.vector.tensor_copy(
             w2_c[:].bitcast(U16), w2_raw[:].bitcast(U16).rearrange("p a (m t) -> p a t m", t=PACK)
         )
-        nc.vector.tensor_copy(w2_sc[:], w2_sc_raw[:].rearrange("p a (m t) -> p a t m", t=PACK))
+        nc.vector.tensor_copy(w2_sc[:], w2_sc_raw.rearrange("p a (m t) -> p a t m", t=PACK))
 
         w1_c = [keep.tile([P, H], U32, name=f"w1_c{a}", align_bytes=64) for a in range(PASSES)]
         w1_sc = [keep.tile([P, H], U8, name=f"w1_sc{a}", align_bytes=64) for a in range(PASSES)]
 
-        def quantise_w1(a, t0, t1):
+        def quantise_w1(a, t0, t1, pieces=1):
             n = t1 - t0
             woven = keep.tile([P, n * P * PACK], BF16, name=f"w1_bf{a}_{t0}", tag=f"w1_bf{a}_{t0}", align_bytes=64)
-            nc.scalar.copy(
-                woven[:].rearrange("p (t m j) -> p m t j", t=n, j=PACK),
-                w1_raw[a][:].rearrange("p j (m t) -> p m t j", t=PACK)[:, :, t0:t1, :],
-            )
+            dst = woven[:].rearrange("p (t m j) -> p m t j", t=n, j=PACK)
+            src = w1_raw[a][:].rearrange("p j (m t) -> p m t j", t=PACK)
+            for m0 in range(0, P, P // pieces):
+                rows = slice(m0, m0 + P // pieces)
+                nc.scalar.copy(dst[:, rows], src[:, rows, t0:t1, :])
             nc.vector.quantize_mx(
                 out=w1_c[a][:, t0 * P : t1 * P].bitcast(E4M3), scales=w1_sc[a][:, t0 * P : t1 * P], in_=woven[:]
             )
@@ -140,7 +138,6 @@ def tile_list_bricklaying_jury_scores_kernel(
             words = keep.tile([P, CHUNK], U32, name=f"v1_{c}", tag=tag, align_bytes=64)
             nc.vector.tensor_copy(words[:], tab_w[1][:].indirect(entries(idx, c * CHUNK, CHUNK)))
             v1.append(words)
-        quantise_w1(1, 1, 4)
 
         def v_codes(a, c):
             words = v0[:, c * CHUNK : (c + 1) * CHUNK] if a == 0 else v1[c][:]
@@ -150,24 +147,24 @@ def tile_list_bricklaying_jury_scores_kernel(
             cols = slice(t * P, (t + 1) * P)
             nc.tensor.matmul_mx(
                 out=bank[:], lhsT=w1_c[a][:, cols].bitcast(E4M3), lhsT_scale=w1_sc[a][:, cols],
-                rhs=v_codes(a, c), rhs_scale=v_sc[a][:, c * CHUNK : (c + 1) * CHUNK],
+                rhs=v_codes(a, c), rhs_scale=v_sc[:, a, c * CHUNK : (c + 1) * CHUNK],
                 start=(a == 0), stop=(a == PASSES - 1),
             )
 
         def bend_pass(bank, t, c, a):
             nc.tensor.matmul_mx(
                 out=bank[:], lhsT=w2_c[:, a, t, :].bitcast(E2M1), lhsT_scale=w2_sc[:, a, t, :],
-                rhs=v_codes(a, c), rhs_scale=v_sc[a][:, c * CHUNK : (c + 1) * CHUNK],
+                rhs=v_codes(a, c), rhs_scale=v_sc[:, a, c * CHUNK : (c + 1) * CHUNK],
                 start=(a == 0), stop=(a == PASSES - 1),
             )
 
         h = [keep.tile([P, S], F32, name=f"h{t}") for t in range(PACK)]
-        a1 = [keep.tile([P, A], F32, name=f"a1_{t}") for t in range(PACK)]
-        a2 = [keep.tile([P, B], F32, name=f"a2_{t}") for t in range(PACK)]
+        a1 = {}
+        a2 = {}
         b4 = keep.tile([P, PACK, C], F32, name="b4")
         a34 = keep.tile([P, PACK, C], F32, name="a34")
 
-        def first_stage(t):
+        def first_products(t):
             marks = [psum.tile([P, CHUNK], F32, name=f"mark{c}", tag=f"mark{c}") for c in range(CHUNKS)]
             bends = [psum.tile([P, CHUNK], F32, name=f"bend{c}", tag=f"bend{c}") for c in range(CHUNKS)]
             if t == 0:
@@ -178,63 +175,88 @@ def tile_list_bricklaying_jury_scores_kernel(
                 bend_pass(bends[c], t, c, a)
                 mark_pass(marks[c], t, c, a)
                 if a == PASSES - 1:
-                    th = ring.tile([P, CHUNK], F32, name="th")
+                    if (t, c) == (PACK - 1, CHUNKS - 1):
+                        th = keep.tile([P, CHUNK], F32, name="th_last", tag="a1_1", align_bytes=64)
+                    else:
+                        th = ring.tile([P, CHUNK], F32, name="th", tag="th")
                     nc.scalar.activation(th[:], bends[c][:], ACT.Tanh)
-                    nc.vector.tensor_tensor(h[t][:, c * CHUNK : (c + 1) * CHUNK], marks[c][:], th[:], ALU.mult)
+                    if t * CHUNKS + c < VECTOR_GATES:
+                        nc.vector.tensor_tensor(h[t][:, c * CHUNK : (c + 1) * CHUNK], marks[c][:], th[:], ALU.mult)
+                    else:
+                        if (t, c) == (PACK - 1, CHUNKS - 1):
+                            mk = keep.tile([P, CHUNK], F32, name="mk_last", tag="a1_0", align_bytes=64)
+                        elif (t, c) == (PACK - 1, 1):
+                            mk = keep.tile([P, CHUNK], F32, name="mk_late", tag="w3_bf", align_bytes=64)
+                        else:
+                            mk = ring.tile([P, CHUNK], F32, name="mk", tag="mk")
+                        nc.scalar.copy(mk[:], marks[c][:])
+                        nc.gpsimd.tensor_tensor(h[t][:, c * CHUNK : (c + 1) * CHUNK], mk[:], th[:], ALU.mult)
 
-        def level_one(t):
-            half = A // 2
-            firsts = []
+        half = A // 2
+        courses = {}
+
+        def level_one_pick(t):
             for u in range(2):
-                first = ring.tile([P, half], F32, name="first")
+                first = keep.tile([P, half], F32, name=f"first{t}_{u}", tag=f"first{t}_{u}", align_bytes=64)
+                second = keep.tile([P, half], F32, name=f"second{t}_{u}", tag=f"second{t}_{u}", align_bytes=64)
                 nc.vector.tensor_copy(first[:], h[t][:].indirect(entries(p1, u * half, half)))
-                firsts.append(first)
+                nc.vector.tensor_copy(second[:], h[t][:].indirect(entries(p2, u * half, half)))
+                courses[t, u] = (first, second)
+
+        def level_one_add(t):
+            a1[t] = keep.tile([P, A], F32, name=f"a1_{t}", tag="first0_1" if t == 2 else f"a1_{t}", align_bytes=64)
             for u in range(2):
-                nc.vector.tensor_tensor(
-                    a1[t][:, u * half : (u + 1) * half], h[t][:].indirect(entries(p2, u * half, half)), firsts[u][:], ALU.add
-                )
+                first, second = courses[t, u]
+                nc.gpsimd.tensor_tensor(a1[t][:, u * half : (u + 1) * half], first[:], second[:], ALU.add)
 
         walls = {}
 
         def level_two_pick(t):
-            left = ring.tile([P, B], F32, name="left")
-            right = ring.tile([P, B], F32, name="right")
+            left = ring.tile([P, B], F32, name="left", tag="left")
+            right = ring.tile([P, B], F32, name="right", tag="right")
             nc.vector.tensor_copy(left[:], a1[t][:].indirect(p3[:]))
             nc.vector.tensor_copy(right[:], a1[t][:].indirect(p4[:]))
             walls[t] = (left, right)
 
         def level_two_max(t):
             left, right = walls[t]
+            a2[t] = keep.tile([P, B], F32, name=f"a2_{t}", tag=("first", "second")[t % 2] + f"{PACK - 1}_{t // 2}", align_bytes=64)
             nc.vector.tensor_tensor(a2[t][:], left[:], right[:], ALU.max)
 
-        first_stage(0)
-        for t in range(PACK):
-            level_one(t)
-            if t + 1 < PACK:
-                first_stage(t + 1)
-            if t > 0:
-                level_two_max(t - 1)
-            level_two_pick(t)
-            if t == 1:
-                w3_bf = keep.tile([P, N * PACK], BF16, name="w3_bf", align_bytes=64)
-                nc.scalar.copy(
-                    w3_bf[:].rearrange("p (c i j) -> p c j i", i=4, j=PACK),
-                    w3_raw[:].rearrange("p j (c i) -> p c j i", i=4),
-                )
-                w3_c = keep.tile([P, N], U32, name="w3_c", align_bytes=64)
-                w3_sc = keep.tile([P, N], U8, name="w3_sc", align_bytes=64)
-                nc.vector.quantize_mx(out=w3_c[:].bitcast(E4M3), scales=w3_sc[:], in_=w3_bf[:])
-
-        for t in range(PACK):
-            if t == PACK - 1:
-                level_two_max(t)
+        def first_competitor(t):
             nc.vector.tensor_copy(b4[:, t, :], a2[t][:].indirect(p5[:]))
+
+        def competitors_product(t):
+            nc.vector.tensor_tensor(a34[:, t, :], a2[t][:].indirect(p6[:]), b4[:, t, :], ALU.mult)
+
+        first_products(0)
+        quantise_w1(1, 1, 4, pieces=4)
+        for t in range(1, PACK):
+            first_products(t)
+        w3_bf = keep.tile([P, N * PACK], BF16, name="w3_bf", tag="w3_bf", align_bytes=64)
+        nc.scalar.copy(
+            w3_bf[:].rearrange("p (c i j) -> p c j i", i=4, j=PACK),
+            w3_raw[:].rearrange("p j (c i) -> p c j i", i=4),
+        )
+        for t in range(PACK):
+            level_one_pick(t)
+        for t in range(PACK):
+            level_one_add(t)
+        for t in range(PACK):
+            level_two_pick(t)
+        for t in range(PACK):
+            level_two_max(t)
+        for t in range(PACK):
+            first_competitor(t)
         b_bf = keep.tile([P, C * PACK], BF16, name="b_bf", align_bytes=64)
         nc.scalar.copy(
             b_bf[:].rearrange("p (c i t) -> p c t i", i=4, t=PACK), b4[:].rearrange("p t (c i) -> p c t i", i=4)
         )
+        w3_c = keep.tile([P, N], U32, name="w3_c", tag=f"a1_{PACK - 1}", align_bytes=64)
+        w3_sc = keep.tile([P, N], U8, name="w3_sc", align_bytes=64)
+        nc.vector.quantize_mx(out=w3_c[:].bitcast(E4M3), scales=w3_sc[:], in_=w3_bf[:])
         for t in range(PACK):
-            nc.vector.tensor_tensor(a34[:, t, :], a2[t][:].indirect(p6[:]), b4[:, t, :], ALU.mult)
+            competitors_product(t)
         b_c = keep.tile([P, C], U32, name="b_c", align_bytes=64)
         b_sc = keep.tile([P, C], U8, name="b_sc", align_bytes=64)
         a3_bf = keep.tile([P, C * PACK], BF16, name="a3_bf", align_bytes=64)
@@ -269,22 +291,22 @@ def tile_list_bricklaying_jury_scores_kernel(
             )
         turns, wholes, fracs, sines = [], [], [], []
         for m in range(tiles):
-            turn = ring.tile([P, C], F32, name="turn")
+            turn = ring.tile([P, C], F32, name="turn", tag="th")
             nc.scalar.activation(turn[:], ys[m][:], ACT.Copy, scale=1.0 / (2.0 * math.pi))
             turns.append(turn)
         for m in range(tiles):
-            whole = ring.tile([P, C], I32, name="whole")
+            whole = ring.tile([P, C], I32, name="whole", tag="mk")
             nc.vector.tensor_scalar(whole[:], turns[m][:], ROUNDER, ROUNDER, ALU.add, ALU.subtract)
             wholes.append(whole)
             if m > 0:
-                frac = ring.tile([P, C], F32, name="frac")
+                frac = ring.tile([P, C], F32, name="frac", tag="left")
                 nc.vector.tensor_tensor(frac[:], turns[m - 1][:], wholes[m - 1][:], ALU.subtract)
                 fracs.append(frac)
-        frac = ring.tile([P, C], F32, name="frac")
+        frac = ring.tile([P, C], F32, name="frac", tag="left")
         nc.vector.tensor_tensor(frac[:], turns[tiles - 1][:], wholes[tiles - 1][:], ALU.subtract)
         fracs.append(frac)
         for m in range(tiles):
-            sine = ring.tile([P, C], F32, name="sine")
+            sine = ring.tile([P, C], F32, name="sine", tag="right")
             nc.scalar.activation(sine[:], fracs[m][:], ACT.Sin, scale=2.0 * math.pi)
             score = ring.tile([P, C], F32, name="score")
             nc.vector.tensor_tensor(score[:], juries[m][:], sine[:], ALU.mult)

@@ -23,7 +23,7 @@ PASSES = K // (P * PACK)
 CHUNK = 512
 CHUNKS = S // CHUNK
 LIST_ROWS = 16
-VECTOR_GATES = 6
+VECTOR_GATES = 5
 ROUNDER = 1.5 * 2.0**23
 
 
@@ -56,88 +56,95 @@ def tile_list_bricklaying_jury_scores_kernel(
         idx = load_list("idx", offs)
         tab_sc = keep.tile([P, T], U8, name="tab_sc", tag="tab_sc", align_bytes=64)
         nc.sync.dma_start(tab_sc[96:128, :].bitcast(I32), tab_scales.rearrange("a q t -> (a q) t").bitcast(I32))
-        w_sc = keep.tile([P, PASSES + 2, H], U8, name="w_sc", align_bytes=64)
-        nc.vector.memset(w_sc[:].rearrange("p a n -> p (a n)").bitcast(I32), 0)
         nc.vector.memset(tab_sc[0:96, :].bitcast(I32), 0)
+        w2_sc_raw = keep.tile([P, PASSES, H], U8, name="w2_sc_raw", tag="w_sc", align_bytes=64)
+        nc.gpsimd.memset(w2_sc_raw[:].rearrange("p a n -> p (a n)").bitcast(I32), 0)
+        load_scale_rows(nc.gpsimd, w2_sc_raw, w2_scales)
         v_sc = keep.tile([P, PASSES, S], U8, name="v_sc", align_bytes=64)
         nc.vector.memset(v_sc[:].rearrange("p a n -> p (a n)").bitcast(I32), 0)
-        w2_sc_raw = w_sc[:, 0:PASSES, :]
-        w4_sc = w_sc[:, PASSES : PASSES + 1, :]
-        w5_sc = w_sc[:, PASSES + 1 : PASSES + 2, :]
-        load_scale_rows(nc.scalar, w2_sc_raw, w2_scales)
 
-        tab_w = [keep.tile([P, T], U32, name=f"tab_w{a}", tag=f"tab_w{a}", align_bytes=64) for a in range(PASSES)]
-        w1_raw = [keep.tile([P, PACK, H], F32, name=f"w1_raw{a}") for a in range(PASSES)]
-        w2_raw = keep.tile([P, PASSES, 2 * H], U8, name="w2_raw", align_bytes=64)
+        def load_table(a, tag):
+            words = keep.tile([P, T], U32, name=f"tab_w{a}", tag=tag, align_bytes=64)
+            nc.sync.dma_start(words[:].bitcast(I32), tab_words[a].rearrange("p t i -> p (t i)").bitcast(I32))
+            return words
 
-        def load_table(a):
-            nc.sync.dma_start(tab_w[a][:].bitcast(I32), tab_words[a].rearrange("p t i -> p (t i)").bitcast(I32))
+        def load_rows(name, src):
+            raw = keep.tile([P, PACK, src.shape[1]], F32, name=name, tag="raw_rows", align_bytes=64)
+            nc.sync.dma_start(raw[:], src.rearrange("(p j) n -> p j n", j=PACK))
+            return raw
 
-        def load_w1(a):
-            nc.sync.dma_start(w1_raw[a][:], w1[a * 512 : (a + 1) * 512, :].rearrange("(p j) n -> p j n", j=PACK))
-
-        load_table(0)
-        nc.sync.dma_start(w2_raw[:].bitcast(I32), w2_words.rearrange("a p b -> p a b").bitcast(I32))
-        load_w1(0)
-        load_table(1)
-        load_w1(1)
+        tab_w0 = load_table(0, "tab_w0")
         p1 = load_list("p1", pos1)
         p2 = load_list("p2", pos2)
         p3 = load_list("p3", pos3)
         p4 = load_list("p4", pos4)
         p5 = load_list("p5", pos5)
         p6 = load_list("p6", pos6)
-        w3_raw = keep.tile([P, PACK, N], F32, name="w3_raw")
-        nc.sync.dma_start(w3_raw[:], w3.rearrange("(p j) n -> p j n", j=PACK))
-        w4_c = keep.tile([P, N], U32, name="w4_c", align_bytes=64)
-        nc.sync.dma_start(w4_c[:].bitcast(I32), w4_words[0].rearrange("p n i -> p (n i)").bitcast(I32))
-        w5_c = keep.tile([P, 2 * N], U8, name="w5_c", align_bytes=64)
-        nc.sync.dma_start(w5_c[:].bitcast(I32), w5_words[0].bitcast(I32))
-        load_scale_rows(nc.sync, w4_sc, w4_scales)
-        load_scale_rows(nc.sync, w5_sc, w5_scales)
+        w1_raw = {0: load_rows("w1_raw0", w1[0:512, :])}
+        w2_raw = keep.tile([P, PASSES, 2 * H], U8, name="w2_raw", tag="w2_raw", align_bytes=64)
+        nc.sync.dma_start(w2_raw[:].bitcast(I32), w2_words.rearrange("a p b -> p a b").bitcast(I32))
 
         picked_sc = keep.tile([P, S], U8, name="picked_sc", align_bytes=64)
         nc.vector.tensor_copy(picked_sc[:], tab_sc[:].indirect(idx[:]))
         for a in range(PASSES):
             for q in range(4):
                 row = 96 + 16 * a + 4 * q
-                nc.gpsimd.dma_start(v_sc[32 * q : 32 * q + 4, a, :].bitcast(I32), picked_sc[row : row + 4, :].bitcast(I32))
+                queue = nc.sync if a == 0 else nc.gpsimd
+                queue.dma_start(v_sc[32 * q : 32 * q + 4, a, :].bitcast(I32), picked_sc[row : row + 4, :].bitcast(I32))
 
+        tab_w1 = load_table(1, "tab_sc")
         v0 = keep.tile([P, S], U32, name="v0", align_bytes=64)
-        nc.vector.tensor_copy(v0[:], tab_w[0][:].indirect(idx[:]))
+        nc.vector.tensor_copy(v0[:], tab_w0[:].indirect(idx[:]))
 
         w2_c = keep.tile([P, PASSES, PACK, 2 * P], U8, name="w2_c", tag="tab_w0", align_bytes=64)
-        w2_sc = keep.tile([P, PASSES, PACK, P], U8, name="w2_sc", tag="tab_sc", align_bytes=64)
         nc.vector.tensor_copy(
             w2_c[:].bitcast(U16), w2_raw[:].bitcast(U16).rearrange("p a (m t) -> p a t m", t=PACK)
         )
+        w2_sc = keep.tile([P, PASSES, PACK, P], U8, name="w2_sc", tag="w2_raw", align_bytes=64)
         nc.vector.tensor_copy(w2_sc[:], w2_sc_raw.rearrange("p a (m t) -> p a t m", t=PACK))
 
         w1_c = [keep.tile([P, H], U32, name=f"w1_c{a}", align_bytes=64) for a in range(PASSES)]
         w1_sc = [keep.tile([P, H], U8, name=f"w1_sc{a}", align_bytes=64) for a in range(PASSES)]
 
-        def quantise_w1(a, t0, t1, pieces=1):
+        def weave_w1(a, t0, t1):
             n = t1 - t0
             woven = keep.tile([P, n * P * PACK], BF16, name=f"w1_bf{a}_{t0}", tag=f"w1_bf{a}_{t0}", align_bytes=64)
             dst = woven[:].rearrange("p (t m j) -> p m t j", t=n, j=PACK)
-            src = w1_raw[a][:].rearrange("p j (m t) -> p m t j", t=PACK)
-            for m0 in range(0, P, P // pieces):
-                rows = slice(m0, m0 + P // pieces)
-                nc.scalar.copy(dst[:, rows], src[:, rows, t0:t1, :])
+            src = w1_raw[a][:].rearrange("p j (m t) -> p m t j", t=PACK)[:, :, t0:t1, :]
+            if t0 == 0:
+                nc.scalar.copy(dst, src)
+            else:
+                nc.gpsimd.tensor_scalar(dst, src, 1.0, 0.0, ALU.mult, ALU.add)
+            return woven
+
+        def quantise_w1(a, t0, t1):
+            woven = weave_w1(a, t0, t1)
             nc.vector.quantize_mx(
                 out=w1_c[a][:, t0 * P : t1 * P].bitcast(E4M3), scales=w1_sc[a][:, t0 * P : t1 * P], in_=woven[:]
             )
 
         quantise_w1(0, 0, 4)
+        w1_raw[1] = load_rows("w1_raw1", w1[512:1024, :])
 
         v1 = []
         for c in range(CHUNKS):
             if c == CHUNKS - 1:
-                quantise_w1(1, 0, 1)
+                quantise_w1(1, 0, 2)
             tag = "w1_bf1_0" if c == CHUNKS - 1 else f"v1_{c}"
             words = keep.tile([P, CHUNK], U32, name=f"v1_{c}", tag=tag, align_bytes=64)
-            nc.vector.tensor_copy(words[:], tab_w[1][:].indirect(entries(idx, c * CHUNK, CHUNK)))
+            nc.vector.tensor_copy(words[:], tab_w1[:].indirect(entries(idx, c * CHUNK, CHUNK)))
             v1.append(words)
+
+        quantise_w1(1, 2, 4)
+
+        w3_raw = load_rows("w3_raw", w3)
+        w4_c = keep.tile([P, N], U32, name="w4_c", tag="w1_bf0_0", align_bytes=64)
+        nc.sync.dma_start(w4_c[:].bitcast(I32), w4_words[0].rearrange("p n i -> p (n i)").bitcast(I32))
+        w45_sc = keep.tile([P, 2, N], U8, name="w45_sc", tag="tab_sc", align_bytes=64)
+        nc.gpsimd.memset(w45_sc[:].rearrange("p a n -> p (a n)").bitcast(I32), 0)
+        w4_sc, w5_sc = w45_sc[:, 0:1, :], w45_sc[:, 1:2, :]
+        load_scale_rows(nc.sync, w4_sc, w4_scales)
+        load_scale_rows(nc.sync, w5_sc, w5_scales)
 
         def v_codes(a, c):
             words = v0[:, c * CHUNK : (c + 1) * CHUNK] if a == 0 else v1[c][:]
@@ -162,7 +169,7 @@ def tile_list_bricklaying_jury_scores_kernel(
         a1 = {}
         a2 = {}
         b4 = keep.tile([P, PACK, C], F32, name="b4")
-        a34 = keep.tile([P, PACK, C], F32, name="a34")
+        a34 = {}
 
         def first_products(t):
             marks = [psum.tile([P, CHUNK], F32, name=f"mark{c}", tag=f"mark{c}") for c in range(CHUNKS)]
@@ -177,6 +184,10 @@ def tile_list_bricklaying_jury_scores_kernel(
                 if a == PASSES - 1:
                     if (t, c) == (PACK - 1, CHUNKS - 1):
                         th = keep.tile([P, CHUNK], F32, name="th_last", tag="a1_1", align_bytes=64)
+                    elif (t, c) == (1, 0):
+                        th = keep.tile([P, CHUNK], F32, name="th_second", tag="second0", align_bytes=64)
+                    elif (t, c) == (0, CHUNKS - 2):
+                        th = keep.tile([P, CHUNK], F32, name="th_first", tag="w1_bf1_2", align_bytes=64)
                     else:
                         th = ring.tile([P, CHUNK], F32, name="th", tag="th")
                     nc.scalar.activation(th[:], bends[c][:], ACT.Tanh)
@@ -192,22 +203,19 @@ def tile_list_bricklaying_jury_scores_kernel(
                         nc.scalar.copy(mk[:], marks[c][:])
                         nc.gpsimd.tensor_tensor(h[t][:, c * CHUNK : (c + 1) * CHUNK], mk[:], th[:], ALU.mult)
 
-        half = A // 2
         courses = {}
 
         def level_one_pick(t):
-            for u in range(2):
-                first = keep.tile([P, half], F32, name=f"first{t}_{u}", tag=f"first{t}_{u}", align_bytes=64)
-                second = keep.tile([P, half], F32, name=f"second{t}_{u}", tag=f"second{t}_{u}", align_bytes=64)
-                nc.vector.tensor_copy(first[:], h[t][:].indirect(entries(p1, u * half, half)))
-                nc.vector.tensor_copy(second[:], h[t][:].indirect(entries(p2, u * half, half)))
-                courses[t, u] = (first, second)
+            first = keep.tile([P, A], F32, name=f"first{t}", tag=f"first{t}", align_bytes=64)
+            second = keep.tile([P, A], F32, name=f"second{t}", tag=f"second{t}", align_bytes=64)
+            nc.vector.tensor_copy(first[:], h[t][:].indirect(p1[:]))
+            nc.vector.tensor_copy(second[:], h[t][:].indirect(p2[:]))
+            courses[t] = (first, second)
 
         def level_one_add(t):
-            a1[t] = keep.tile([P, A], F32, name=f"a1_{t}", tag="first0_1" if t == 2 else f"a1_{t}", align_bytes=64)
-            for u in range(2):
-                first, second = courses[t, u]
-                nc.gpsimd.tensor_tensor(a1[t][:, u * half : (u + 1) * half], first[:], second[:], ALU.add)
+            a1[t] = keep.tile([P, A], F32, name=f"a1_{t}", tag="first0" if t == 2 else f"a1_{t}", align_bytes=64)
+            first, second = courses[t]
+            nc.gpsimd.tensor_tensor(a1[t][:], first[:], second[:], ALU.add)
 
         walls = {}
 
@@ -220,17 +228,18 @@ def tile_list_bricklaying_jury_scores_kernel(
 
         def level_two_max(t):
             left, right = walls[t]
-            a2[t] = keep.tile([P, B], F32, name=f"a2_{t}", tag=("first", "second")[t % 2] + f"{PACK - 1}_{t // 2}", align_bytes=64)
+            a2[t] = keep.tile([P, B], F32, name=f"a2_{t}", tag=(f"first{PACK - 1}", f"second{PACK - 1}", "a2_2", "a2_3")[t], align_bytes=64)
             nc.vector.tensor_tensor(a2[t][:], left[:], right[:], ALU.max)
 
         def first_competitor(t):
             nc.vector.tensor_copy(b4[:, t, :], a2[t][:].indirect(p5[:]))
 
-        def competitors_product(t):
-            nc.vector.tensor_tensor(a34[:, t, :], a2[t][:].indirect(p6[:]), b4[:, t, :], ALU.mult)
+        def competitors_product(t, u):
+            nc.vector.tensor_tensor(
+                a34[u][:, t, :], a2[t][:].indirect(entries(p6, u * P, P)), b4[:, t, u * P : (u + 1) * P], ALU.mult
+            )
 
         first_products(0)
-        quantise_w1(1, 1, 4, pieces=4)
         for t in range(1, PACK):
             first_products(t)
         w3_bf = keep.tile([P, N * PACK], BF16, name="w3_bf", tag="w3_bf", align_bytes=64)
@@ -238,6 +247,8 @@ def tile_list_bricklaying_jury_scores_kernel(
             w3_bf[:].rearrange("p (c i j) -> p c j i", i=4, j=PACK),
             w3_raw[:].rearrange("p j (c i) -> p c j i", i=4),
         )
+        w5_c = keep.tile([P, 2 * N], U8, name="w5_c", tag="raw_rows", align_bytes=64)
+        nc.sync.dma_start(w5_c[:].bitcast(I32), w5_words[0].bitcast(I32))
         for t in range(PACK):
             level_one_pick(t)
         for t in range(PACK):
@@ -248,66 +259,99 @@ def tile_list_bricklaying_jury_scores_kernel(
             level_two_max(t)
         for t in range(PACK):
             first_competitor(t)
-        b_bf = keep.tile([P, C * PACK], BF16, name="b_bf", align_bytes=64)
+        b_bf = keep.tile([P, C * PACK], BF16, name="b_bf", tag="b_bf", align_bytes=64)
         nc.scalar.copy(
             b_bf[:].rearrange("p (c i t) -> p c t i", i=4, t=PACK), b4[:].rearrange("p t (c i) -> p c t i", i=4)
         )
         w3_c = keep.tile([P, N], U32, name="w3_c", tag=f"a1_{PACK - 1}", align_bytes=64)
         w3_sc = keep.tile([P, N], U8, name="w3_sc", align_bytes=64)
         nc.vector.quantize_mx(out=w3_c[:].bitcast(E4M3), scales=w3_sc[:], in_=w3_bf[:])
-        for t in range(PACK):
-            competitors_product(t)
         b_c = keep.tile([P, C], U32, name="b_c", align_bytes=64)
         b_sc = keep.tile([P, C], U8, name="b_sc", align_bytes=64)
-        a3_bf = keep.tile([P, C * PACK], BF16, name="a3_bf", align_bytes=64)
-        nc.vector.tensor_copy(
-            a3_bf[:].rearrange("p (c i t) -> p c t i", i=4, t=PACK), a34[:].rearrange("p t (c i) -> p c t i", i=4)
-        )
-        nc.vector.quantize_mx(out=b_c[:].bitcast(E4M3), scales=b_sc[:], in_=b_bf[:])
-        a3_c = keep.tile([P, C], U32, name="a3_c", align_bytes=64)
-        a3_sc = keep.tile([P, C], U8, name="a3_sc", align_bytes=64)
-        nc.vector.quantize_mx(out=a3_c[:].bitcast(E4M3), scales=a3_sc[:], in_=a3_bf[:])
+        a3_bf, a3_c, a3_sc = {}, {}, {}
 
-        tiles = N // P
-        ys = [psum.tile([P, C], F32, name=f"y{m}", tag=f"mark{m}") for m in range(tiles)]
-        juries = [psum.tile([P, C], F32, name=f"jury{m}", tag=f"bend{m}") for m in range(tiles)]
-        for m in range(tiles):
-            cols = slice(m * P, (m + 1) * P)
-            nc.tensor.matmul_mx(
-                out=ys[m][:], lhsT=w4_c[:, cols].bitcast(E4M3), lhsT_scale=w4_sc[:, 0, cols],
-                rhs=b_c[:].bitcast(E4M3), rhs_scale=b_sc[:], start=True, stop=False,
+        def weave_a3(u):
+            a3_bf[u] = keep.tile([P, P * PACK], BF16, name=f"a3_bf{u}", align_bytes=64)
+            nc.scalar.copy(
+                a3_bf[u][:].rearrange("p (c i t) -> p c t i", i=4, t=PACK),
+                a34[u][:].rearrange("p t (c i) -> p c t i", i=4),
             )
-        for m in range(tiles):
-            cols = slice(m * P, (m + 1) * P)
-            nc.tensor.matmul_mx(
-                out=ys[m][:], lhsT=w3_c[:, cols].bitcast(E4M3), lhsT_scale=w3_sc[:, cols],
-                rhs=a3_c[:].bitcast(E4M3), rhs_scale=a3_sc[:], start=False, stop=True,
-            )
-        for m in range(tiles):
-            nc.tensor.matmul_mx(
-                out=juries[m][:], lhsT=w5_c[:, 2 * m * P : 2 * (m + 1) * P].bitcast(E2M1),
-                lhsT_scale=w5_sc[:, 0, m * P : (m + 1) * P],
-                rhs=a3_c[:].bitcast(E4M3), rhs_scale=a3_sc[:], start=True, stop=True,
-            )
-        turns, wholes, fracs, sines = [], [], [], []
-        for m in range(tiles):
-            turn = ring.tile([P, C], F32, name="turn", tag="th")
-            nc.scalar.activation(turn[:], ys[m][:], ACT.Copy, scale=1.0 / (2.0 * math.pi))
-            turns.append(turn)
-        for m in range(tiles):
-            whole = ring.tile([P, C], I32, name="whole", tag="mk")
-            nc.vector.tensor_scalar(whole[:], turns[m][:], ROUNDER, ROUNDER, ALU.add, ALU.subtract)
-            wholes.append(whole)
-            if m > 0:
-                frac = ring.tile([P, C], F32, name="frac", tag="left")
-                nc.vector.tensor_tensor(frac[:], turns[m - 1][:], wholes[m - 1][:], ALU.subtract)
-                fracs.append(frac)
-        frac = ring.tile([P, C], F32, name="frac", tag="left")
-        nc.vector.tensor_tensor(frac[:], turns[tiles - 1][:], wholes[tiles - 1][:], ALU.subtract)
-        fracs.append(frac)
-        for m in range(tiles):
-            sine = ring.tile([P, C], F32, name="sine", tag="right")
-            nc.scalar.activation(sine[:], fracs[m][:], ACT.Sin, scale=2.0 * math.pi)
-            score = ring.tile([P, C], F32, name="score")
-            nc.vector.tensor_tensor(score[:], juries[m][:], sine[:], ALU.mult)
-            nc.sync.dma_start(out[m * P : (m + 1) * P, :], score[:])
+
+        def quantise_a3(u):
+            a3_c[u] = keep.tile([P, P], U32, name=f"a3_c{u}", align_bytes=64)
+            a3_sc[u] = keep.tile([P, P], U8, name=f"a3_sc{u}", align_bytes=64)
+            nc.vector.quantize_mx(out=a3_c[u][:].bitcast(E4M3), scales=a3_sc[u][:], in_=a3_bf[u][:])
+
+        ys, juries, turns, wholes, fracs = {}, {}, {}, {}, {}
+
+        def open_y(u, g):
+            ys[u, g] = psum.tile([P, 2, P], F32, name=f"y{u}{g}", tag=f"mark{2 * u + g}")
+            for i in range(2):
+                cols = slice((2 * g + i) * P, (2 * g + i + 1) * P)
+                nc.tensor.matmul_mx(
+                    out=ys[u, g][:, i, :], lhsT=w4_c[:, cols].bitcast(E4M3), lhsT_scale=w4_sc[:, 0, cols],
+                    rhs=b_c[:, u * P : (u + 1) * P].bitcast(E4M3), rhs_scale=b_sc[:, u * P : (u + 1) * P],
+                    start=(i == 0), stop=False,
+                )
+
+        def close_y(u, g):
+            for i in range(2):
+                cols = slice((2 * g + i) * P, (2 * g + i + 1) * P)
+                nc.tensor.matmul_mx(
+                    out=ys[u, g][:, i, :], lhsT=w3_c[:, cols].bitcast(E4M3), lhsT_scale=w3_sc[:, cols],
+                    rhs=a3_c[u][:].bitcast(E4M3), rhs_scale=a3_sc[u][:], start=False, stop=(i == 1),
+                )
+
+        def jury_product(u, g):
+            juries[u, g] = psum.tile([P, 2, P], F32, name=f"jury{u}{g}", tag=f"bend{2 * u + g}")
+            for i in range(2):
+                m = 2 * g + i
+                nc.tensor.matmul_mx(
+                    out=juries[u, g][:, i, :], lhsT=w5_c[:, 2 * m * P : 2 * (m + 1) * P].bitcast(E2M1),
+                    lhsT_scale=w5_sc[:, 0, m * P : (m + 1) * P],
+                    rhs=a3_c[u][:].bitcast(E4M3), rhs_scale=a3_sc[u][:], start=True, stop=True,
+                )
+
+        def reduce_angle(u):
+            for g in range(2):
+                turns[g] = ring.tile([P, 2, P], F32, name="turn", tag="th")
+                nc.scalar.activation(turns[g][:], ys[u, g][:], ACT.Copy, scale=1.0 / (2.0 * math.pi))
+            for g in range(2):
+                wholes[g] = ring.tile([P, 2, P], I32, name="whole", tag="mk")
+                nc.vector.tensor_scalar(wholes[g][:], turns[g][:], ROUNDER, ROUNDER, ALU.add, ALU.subtract)
+            for g in range(2):
+                fracs[u, g] = ring.tile([P, 2, P], F32, name="frac", tag="left")
+                nc.vector.tensor_tensor(fracs[u, g][:], turns[g][:], wholes[g][:], ALU.subtract)
+
+        def finish(u):
+            for g in range(2):
+                sine = ring.tile([P, 2, P], F32, name="sine", tag="right")
+                nc.scalar.activation(sine[:], fracs[u, g][:], ACT.Sin, scale=2.0 * math.pi)
+                score = ring.tile([P, 2, P], F32, name="score")
+                nc.vector.tensor_tensor(score[:], juries[u, g][:], sine[:], ALU.mult)
+                rows = out[2 * g * P : 2 * (g + 1) * P, u * P : (u + 1) * P]
+                nc.sync.dma_start(rows.rearrange("(i p) c -> p i c", i=2), score[:])
+
+        a34[0] = keep.tile([P, PACK, P], F32, name="a34_0")
+        for t in range(PACK):
+            competitors_product(t, 0)
+        weave_a3(0)
+        nc.vector.quantize_mx(out=b_c[:].bitcast(E4M3), scales=b_sc[:], in_=b_bf[:])
+        for u in range(2):
+            for g in range(2):
+                open_y(u, g)
+        a34[1] = keep.tile([P, PACK, P], F32, name="a34_1", tag="b_bf", align_bytes=64)
+        for t in range(PACK):
+            competitors_product(t, 1)
+        weave_a3(1)
+        for u in range(2):
+            quantise_a3(u)
+            for g in range(2):
+                close_y(u, g)
+        for u in range(2):
+            for g in range(2):
+                jury_product(u, g)
+        for u in range(2):
+            reduce_angle(u)
+        for u in range(2):
+            finish(u)

@@ -73,6 +73,10 @@ def tile_list_bricklaying_jury_scores_kernel(
             nc.sync.dma_start(raw[:], src.rearrange("(p j) n -> p j n", j=PACK))
             return raw
 
+        warm_in = keep.tile([P, 8], F32, name="warm_in")
+        warm_out = keep.tile([P, 8], F32, name="warm_out")
+        nc.gpsimd.memset(warm_in[:], 0.0)
+        nc.scalar.activation(warm_out[:], warm_in[:], ACT.Silu)
         tab_w0 = load_table(0, "tab_w0")
         p1 = load_list("p1", pos1)
         p2 = load_list("p2", pos2)

@@ -4,7 +4,7 @@ from contextlib import ExitStack
 import concourse.mybir as mybir
 
 K, H, N, T, S, A, B, C = 1024, 512, 512, 4096, 2048, 1024, 512, 256
-FLOPS = 4697620480
+FLOPS = 2 * (2 * K * H * S + 3 * H * N * C)
 
 F32 = mybir.dt.float32
 BF16 = mybir.dt.bfloat16
@@ -19,10 +19,18 @@ ACT = mybir.ActivationFunctionType
 
 P = 128
 PACK = 4
-PASSES = K // (P * PACK)
+LAST = PACK - 1
+K_PASS = P * PACK
+PASSES = K // K_PASS
+QUADRANTS = 4
+SCALE_ROWS = 16
+TABLE_SCALES_AT = P - PASSES * SCALE_ROWS
 CHUNK = 512
 CHUNKS = S // CHUNK
 LIST_ROWS = 16
+RUN = 4
+HALVES = C // P
+PAIRS = N // (2 * P)
 VECTOR_GATES = 5
 ROUNDER = 1.5 * 2.0**23
 
@@ -39,44 +47,51 @@ def tile_list_bricklaying_jury_scores_kernel(
         psum = ctx.enter_context(tc.psum_pool(name="psum", bufs=1))
 
         def load_list(name, src):
-            tile = lists.tile([P, src.shape[1]], U16, name=name)
-            nc.sync.dma_start(tile[:], src)
-            return tile
+            offsets = lists.tile([P, src.shape[1]], U16, name=name)
+            nc.sync.dma_start(offsets[:], src)
+            return offsets
 
-        def entries(tile, first, count):
-            return tile[:, first // LIST_ROWS : (first + count) // LIST_ROWS]
+        def entries(offsets, first, count):
+            return offsets[:, first // LIST_ROWS : (first + count) // LIST_ROWS]
 
-        def load_scale_rows(queue, plane, src):
-            for q in range(4):
+        def load_scale_rows(queue, scales, src):
+            for q in range(QUADRANTS):
                 queue.dma_start(
-                    plane[32 * q : 32 * q + 4].bitcast(I32),
-                    src[:, 4 * q : 4 * q + 4, :].rearrange("a r n -> r a n").bitcast(I32),
+                    scales[32 * q : 32 * q + 4].bitcast(I32),
+                    src[:, 4 * q : 4 * q + 4, :].rearrange("a s n -> s a n").bitcast(I32),
                 )
-
-        idx = load_list("idx", offs)
-        tab_sc = keep.tile([P, T], U8, name="tab_sc", tag="tab_sc", align_bytes=64)
-        nc.sync.dma_start(tab_sc[96:128, :].bitcast(I32), tab_scales.rearrange("a q t -> (a q) t").bitcast(I32))
-        nc.vector.memset(tab_sc[0:96, :].bitcast(I32), 0)
-        w2_sc_raw = keep.tile([P, PASSES, H], U8, name="w2_sc_raw", tag="w_sc", align_bytes=64)
-        nc.gpsimd.memset(w2_sc_raw[:].rearrange("p a n -> p (a n)").bitcast(I32), 0)
-        load_scale_rows(nc.gpsimd, w2_sc_raw, w2_scales)
-        v_sc = keep.tile([P, PASSES, S], U8, name="v_sc", align_bytes=64)
-        nc.vector.memset(v_sc[:].rearrange("p a n -> p (a n)").bitcast(I32), 0)
 
         def load_table(a, tag):
             words = keep.tile([P, T], U32, name=f"tab_w{a}", tag=tag, align_bytes=64)
             nc.sync.dma_start(words[:].bitcast(I32), tab_words[a].rearrange("p t i -> p (t i)").bitcast(I32))
             return words
 
-        def load_rows(name, src):
-            raw = keep.tile([P, PACK, src.shape[1]], F32, name=name, tag="raw_rows", align_bytes=64)
+        def load_rows(name, src, tag):
+            raw = keep.tile([P, PACK, src.shape[1]], F32, name=name, tag=tag, align_bytes=64)
             nc.sync.dma_start(raw[:], src.rearrange("(p j) n -> p j n", j=PACK))
             return raw
+
+        def interleave(woven, rows):
+            nc.scalar.copy(
+                woven[:].rearrange("p (c i j) -> p c j i", i=RUN, j=PACK),
+                rows[:].rearrange("p j (c i) -> p c j i", i=RUN),
+            )
+
+        idx = load_list("idx", offs)
+        tab_sc = keep.tile([P, T], U8, name="tab_sc", tag="tab_sc", align_bytes=64)
+        nc.sync.dma_start(tab_sc[TABLE_SCALES_AT:P, :].bitcast(I32), tab_scales.rearrange("a q t -> (a q) t").bitcast(I32))
+        nc.vector.memset(tab_sc[0:TABLE_SCALES_AT, :].bitcast(I32), 0)
+        w2_sc_raw = keep.tile([P, PASSES, H], U8, name="w2_sc_raw", align_bytes=64)
+        nc.gpsimd.memset(w2_sc_raw[:].rearrange("p a n -> p (a n)").bitcast(I32), 0)
+        load_scale_rows(nc.gpsimd, w2_sc_raw, w2_scales)
+        v_sc = keep.tile([P, PASSES, S], U8, name="v_sc", align_bytes=64)
+        nc.vector.memset(v_sc[:].rearrange("p a n -> p (a n)").bitcast(I32), 0)
 
         warm_in = keep.tile([P, 8], F32, name="warm_in")
         warm_out = keep.tile([P, 8], F32, name="warm_out")
         nc.gpsimd.memset(warm_in[:], 0.0)
         nc.scalar.activation(warm_out[:], warm_in[:], ACT.Silu)
+
         tab_w0 = load_table(0, "tab_w0")
         p1 = load_list("p1", pos1)
         p2 = load_list("p2", pos2)
@@ -84,16 +99,16 @@ def tile_list_bricklaying_jury_scores_kernel(
         p4 = load_list("p4", pos4)
         p5 = load_list("p5", pos5)
         p6 = load_list("p6", pos6)
-        w1_raw = {0: load_rows("w1_raw0", w1[0:512, :])}
+        w1_raw = [load_rows("w1_raw0", w1[0:K_PASS, :], "raw0")]
         w2_raw = keep.tile([P, PASSES, 2 * H], U8, name="w2_raw", tag="w2_raw", align_bytes=64)
         nc.sync.dma_start(w2_raw[:].bitcast(I32), w2_words.rearrange("a p b -> p a b").bitcast(I32))
+        w1_raw.append(load_rows("w1_raw1", w1[K_PASS:K, :], "raw1"))
 
         picked_sc = keep.tile([P, S], U8, name="picked_sc", align_bytes=64)
         nc.vector.tensor_copy(picked_sc[:], tab_sc[:].indirect(idx[:]))
-        for a in range(PASSES):
-            for q in range(4):
-                row = 96 + 16 * a + 4 * q
-                queue = nc.sync if a == 0 else nc.gpsimd
+        for a, queue in enumerate((nc.sync, nc.gpsimd)):
+            for q in range(QUADRANTS):
+                row = TABLE_SCALES_AT + SCALE_ROWS * a + 4 * q
                 queue.dma_start(v_sc[32 * q : 32 * q + 4, a, :].bitcast(I32), picked_sc[row : row + 4, :].bitcast(I32))
 
         tab_w1 = load_table(1, "tab_sc")
@@ -101,261 +116,178 @@ def tile_list_bricklaying_jury_scores_kernel(
         nc.vector.tensor_copy(v0[:], tab_w0[:].indirect(idx[:]))
 
         w2_c = keep.tile([P, PASSES, PACK, 2 * P], U8, name="w2_c", tag="tab_w0", align_bytes=64)
-        nc.vector.tensor_copy(
-            w2_c[:].bitcast(U16), w2_raw[:].bitcast(U16).rearrange("p a (m t) -> p a t m", t=PACK)
-        )
+        nc.vector.tensor_copy(w2_c[:].bitcast(U16), w2_raw[:].bitcast(U16).rearrange("p a (m t) -> p a t m", t=PACK))
         w2_sc = keep.tile([P, PASSES, PACK, P], U8, name="w2_sc", tag="w2_raw", align_bytes=64)
-        nc.vector.tensor_copy(w2_sc[:], w2_sc_raw.rearrange("p a (m t) -> p a t m", t=PACK))
+        nc.vector.tensor_copy(w2_sc[:], w2_sc_raw[:].rearrange("p a (m t) -> p a t m", t=PACK))
 
         w1_c = [keep.tile([P, H], U32, name=f"w1_c{a}", align_bytes=64) for a in range(PASSES)]
         w1_sc = [keep.tile([P, H], U8, name=f"w1_sc{a}", align_bytes=64) for a in range(PASSES)]
-
-        def weave_w1(a, t0, t1):
-            n = t1 - t0
-            woven = keep.tile([P, n * P * PACK], BF16, name=f"w1_bf{a}_{t0}", tag=f"w1_bf{a}_{t0}", align_bytes=64)
-            dst = woven[:].rearrange("p (t m j) -> p m t j", t=n, j=PACK)
-            src = w1_raw[a][:].rearrange("p j (m t) -> p m t j", t=PACK)[:, :, t0:t1, :]
-            if t0 == 0:
-                nc.scalar.copy(dst, src)
-            else:
-                nc.gpsimd.tensor_scalar(dst, src, 1.0, 0.0, ALU.mult, ALU.add)
-            return woven
-
-        def quantise_w1(a, t0, t1):
-            woven = weave_w1(a, t0, t1)
-            nc.vector.quantize_mx(
-                out=w1_c[a][:, t0 * P : t1 * P].bitcast(E4M3), scales=w1_sc[a][:, t0 * P : t1 * P], in_=woven[:]
+        for a in range(PASSES):
+            w1_bf = keep.tile([P, H * PACK], BF16, name=f"w1_bf{a}", tag=f"w1_bf{a}", align_bytes=64)
+            nc.scalar.copy(
+                w1_bf[:].rearrange("p (t m j) -> p m t j", t=PACK, j=PACK),
+                w1_raw[a][:].rearrange("p j (m t) -> p m t j", t=PACK),
             )
-
-        quantise_w1(0, 0, 4)
-        w1_raw[1] = load_rows("w1_raw1", w1[512:1024, :])
+            nc.vector.quantize_mx(out=w1_c[a][:].bitcast(E4M3), scales=w1_sc[a][:], in_=w1_bf[:])
 
         v1 = []
         for c in range(CHUNKS):
-            if c == CHUNKS - 1:
-                quantise_w1(1, 0, 2)
-            tag = "w1_bf1_0" if c == CHUNKS - 1 else f"v1_{c}"
-            words = keep.tile([P, CHUNK], U32, name=f"v1_{c}", tag=tag, align_bytes=64)
+            words = keep.tile([P, CHUNK], U32, name=f"v1_{c}", align_bytes=64)
             nc.vector.tensor_copy(words[:], tab_w1[:].indirect(entries(idx, c * CHUNK, CHUNK)))
             v1.append(words)
 
-        quantise_w1(1, 2, 4)
-
-        w3_raw = load_rows("w3_raw", w3)
-        w4_c = keep.tile([P, N], U32, name="w4_c", tag="w1_bf0_0", align_bytes=64)
+        w3_raw = load_rows("w3_raw", w3, "raw1")
+        w4_c = keep.tile([P, N], U32, name="w4_c", tag="w1_bf0", align_bytes=64)
         nc.sync.dma_start(w4_c[:].bitcast(I32), w4_words[0].rearrange("p n i -> p (n i)").bitcast(I32))
         w45_sc = keep.tile([P, 2, N], U8, name="w45_sc", tag="tab_sc", align_bytes=64)
-        nc.gpsimd.memset(w45_sc[:].rearrange("p a n -> p (a n)").bitcast(I32), 0)
+        nc.gpsimd.memset(w45_sc[:].rearrange("p w n -> p (w n)").bitcast(I32), 0)
         w4_sc, w5_sc = w45_sc[:, 0:1, :], w45_sc[:, 1:2, :]
         load_scale_rows(nc.sync, w4_sc, w4_scales)
         load_scale_rows(nc.sync, w5_sc, w5_scales)
 
-        def v_codes(a, c):
-            words = v0[:, c * CHUNK : (c + 1) * CHUNK] if a == 0 else v1[c][:]
-            return words.bitcast(E4M3)
-
-        def mark_pass(bank, t, c, a):
-            cols = slice(t * P, (t + 1) * P)
+        def table_pass(bank, codes, scales, c, a):
+            cols = slice(c * CHUNK, (c + 1) * CHUNK)
+            words = v0[:, cols] if a == 0 else v1[c][:]
             nc.tensor.matmul_mx(
-                out=bank[:], lhsT=w1_c[a][:, cols].bitcast(E4M3), lhsT_scale=w1_sc[a][:, cols],
-                rhs=v_codes(a, c), rhs_scale=v_sc[:, a, c * CHUNK : (c + 1) * CHUNK],
+                out=bank[:], lhsT=codes, lhsT_scale=scales, rhs=words.bitcast(E4M3), rhs_scale=v_sc[:, a, cols],
                 start=(a == 0), stop=(a == PASSES - 1),
             )
 
-        def bend_pass(bank, t, c, a):
-            nc.tensor.matmul_mx(
-                out=bank[:], lhsT=w2_c[:, a, t, :].bitcast(E2M1), lhsT_scale=w2_sc[:, a, t, :],
-                rhs=v_codes(a, c), rhs_scale=v_sc[:, a, c * CHUNK : (c + 1) * CHUNK],
-                start=(a == 0), stop=(a == PASSES - 1),
-            )
+        tanh_heir = {(LAST, CHUNKS - 1): "a1_1", divmod(VECTOR_GATES - 1, CHUNKS): "second0"}
+        mark_heir = {(LAST, CHUNKS - 1): "a1_0", (LAST, 1): "w3_bf"}
+
+        def chunk_tile(name, heir):
+            if heir is None:
+                return ring.tile([P, CHUNK], F32, name=name, tag=name)
+            return keep.tile([P, CHUNK], F32, name=f"{name}_{heir}", tag=heir, align_bytes=64)
 
         h = [keep.tile([P, S], F32, name=f"h{t}") for t in range(PACK)]
-        a1 = {}
-        a2 = {}
         b4 = keep.tile([P, PACK, C], F32, name="b4")
-        a34 = {}
-
-        def first_products(t):
+        for t in range(PACK):
             marks = [psum.tile([P, CHUNK], F32, name=f"mark{c}", tag=f"mark{c}") for c in range(CHUNKS)]
             bends = [psum.tile([P, CHUNK], F32, name=f"bend{c}", tag=f"bend{c}") for c in range(CHUNKS)]
             if t == 0:
                 order = [(c, a) for a in range(PASSES) for c in range(CHUNKS)]
             else:
                 order = [(c, a) for c in range(CHUNKS) for a in range(PASSES)]
+            dealt = slice(t * P, (t + 1) * P)
             for c, a in order:
-                bend_pass(bends[c], t, c, a)
-                mark_pass(marks[c], t, c, a)
+                table_pass(bends[c], w2_c[:, a, t, :].bitcast(E2M1), w2_sc[:, a, t, :], c, a)
+                table_pass(marks[c], w1_c[a][:, dealt].bitcast(E4M3), w1_sc[a][:, dealt], c, a)
                 if a == PASSES - 1:
-                    if (t, c) == (PACK - 1, CHUNKS - 1):
-                        th = keep.tile([P, CHUNK], F32, name="th_last", tag="a1_1", align_bytes=64)
-                    elif (t, c) == (1, 0):
-                        th = keep.tile([P, CHUNK], F32, name="th_second", tag="second0", align_bytes=64)
-                    elif (t, c) == (0, CHUNKS - 2):
-                        th = keep.tile([P, CHUNK], F32, name="th_first", tag="w1_bf1_2", align_bytes=64)
-                    else:
-                        th = ring.tile([P, CHUNK], F32, name="th", tag="th")
-                    nc.scalar.activation(th[:], bends[c][:], ACT.Tanh)
+                    gated = h[t][:, c * CHUNK : (c + 1) * CHUNK]
+                    tanh = chunk_tile("tanh", tanh_heir.get((t, c)))
+                    nc.scalar.activation(tanh[:], bends[c][:], ACT.Tanh)
                     if t * CHUNKS + c < VECTOR_GATES:
-                        nc.vector.tensor_tensor(h[t][:, c * CHUNK : (c + 1) * CHUNK], marks[c][:], th[:], ALU.mult)
+                        nc.vector.tensor_tensor(gated, marks[c][:], tanh[:], ALU.mult)
                     else:
-                        if (t, c) == (PACK - 1, CHUNKS - 1):
-                            mk = keep.tile([P, CHUNK], F32, name="mk_last", tag="a1_0", align_bytes=64)
-                        elif (t, c) == (PACK - 1, 1):
-                            mk = keep.tile([P, CHUNK], F32, name="mk_late", tag="w3_bf", align_bytes=64)
-                        else:
-                            mk = ring.tile([P, CHUNK], F32, name="mk", tag="mk")
-                        nc.scalar.copy(mk[:], marks[c][:])
-                        nc.gpsimd.tensor_tensor(h[t][:, c * CHUNK : (c + 1) * CHUNK], mk[:], th[:], ALU.mult)
+                        mark_sb = chunk_tile("mark_sb", mark_heir.get((t, c)))
+                        nc.scalar.copy(mark_sb[:], marks[c][:])
+                        nc.gpsimd.tensor_tensor(gated, mark_sb[:], tanh[:], ALU.mult)
 
-        courses = {}
+        w3_bf = keep.tile([P, N * PACK], BF16, name="w3_bf", tag="w3_bf", align_bytes=64)
+        interleave(w3_bf, w3_raw)
+        w5_c = keep.tile([P, 2 * N], U8, name="w5_c", tag="raw1", align_bytes=64)
+        nc.sync.dma_start(w5_c[:].bitcast(I32), w5_words[0].bitcast(I32))
 
-        def level_one_pick(t):
+        courses = []
+        for t in range(PACK):
             first = keep.tile([P, A], F32, name=f"first{t}", tag=f"first{t}", align_bytes=64)
             second = keep.tile([P, A], F32, name=f"second{t}", tag=f"second{t}", align_bytes=64)
             nc.vector.tensor_copy(first[:], h[t][:].indirect(p1[:]))
             nc.vector.tensor_copy(second[:], h[t][:].indirect(p2[:]))
-            courses[t] = (first, second)
+            courses.append((first, second))
+        a1 = []
+        for t, tag in enumerate(("a1_0", "a1_1", "first0", "a1_3")):
+            a1.append(keep.tile([P, A], F32, name=f"a1_{t}", tag=tag, align_bytes=64))
+            nc.gpsimd.tensor_tensor(a1[t][:], courses[t][0][:], courses[t][1][:], ALU.add)
 
-        def level_one_add(t):
-            a1[t] = keep.tile([P, A], F32, name=f"a1_{t}", tag="first0" if t == 2 else f"a1_{t}", align_bytes=64)
-            first, second = courses[t]
-            nc.gpsimd.tensor_tensor(a1[t][:], first[:], second[:], ALU.add)
-
-        walls = {}
-
-        def level_two_pick(t):
+        walls = []
+        for t in range(PACK):
             left = ring.tile([P, B], F32, name="left", tag="left")
             right = ring.tile([P, B], F32, name="right", tag="right")
             nc.vector.tensor_copy(left[:], a1[t][:].indirect(p3[:]))
             nc.vector.tensor_copy(right[:], a1[t][:].indirect(p4[:]))
-            walls[t] = (left, right)
+            walls.append((left, right))
+        a2 = []
+        for t, tag in enumerate((f"first{LAST}", f"second{LAST}", "a2_2", "a2_3")):
+            a2.append(keep.tile([P, B], F32, name=f"a2_{t}", tag=tag, align_bytes=64))
+            nc.vector.tensor_tensor(a2[t][:], walls[t][0][:], walls[t][1][:], ALU.max)
 
-        def level_two_max(t):
-            left, right = walls[t]
-            a2[t] = keep.tile([P, B], F32, name=f"a2_{t}", tag=(f"first{PACK - 1}", f"second{PACK - 1}", "a2_2", "a2_3")[t], align_bytes=64)
-            nc.vector.tensor_tensor(a2[t][:], left[:], right[:], ALU.max)
-
-        def first_competitor(t):
+        for t in range(PACK):
             nc.vector.tensor_copy(b4[:, t, :], a2[t][:].indirect(p5[:]))
-
-        def competitors_product(t, u):
-            nc.vector.tensor_tensor(
-                a34[u][:, t, :], a2[t][:].indirect(entries(p6, u * P, P)), b4[:, t, u * P : (u + 1) * P], ALU.mult
-            )
-
-        first_products(0)
-        for t in range(1, PACK):
-            first_products(t)
-        w3_bf = keep.tile([P, N * PACK], BF16, name="w3_bf", tag="w3_bf", align_bytes=64)
-        nc.scalar.copy(
-            w3_bf[:].rearrange("p (c i j) -> p c j i", i=4, j=PACK),
-            w3_raw[:].rearrange("p j (c i) -> p c j i", i=4),
-        )
-        w5_c = keep.tile([P, 2 * N], U8, name="w5_c", tag="raw_rows", align_bytes=64)
-        nc.sync.dma_start(w5_c[:].bitcast(I32), w5_words[0].bitcast(I32))
-        for t in range(PACK):
-            level_one_pick(t)
-        for t in range(PACK):
-            level_one_add(t)
-        for t in range(PACK):
-            level_two_pick(t)
-        for t in range(PACK):
-            level_two_max(t)
-        for t in range(PACK):
-            first_competitor(t)
         b_bf = keep.tile([P, C * PACK], BF16, name="b_bf", tag="b_bf", align_bytes=64)
-        nc.scalar.copy(
-            b_bf[:].rearrange("p (c i t) -> p c t i", i=4, t=PACK), b4[:].rearrange("p t (c i) -> p c t i", i=4)
-        )
-        w3_c = keep.tile([P, N], U32, name="w3_c", tag=f"a1_{PACK - 1}", align_bytes=64)
+        interleave(b_bf, b4)
+        w3_c = keep.tile([P, N], U32, name="w3_c", tag="a1_3", align_bytes=64)
         w3_sc = keep.tile([P, N], U8, name="w3_sc", align_bytes=64)
         nc.vector.quantize_mx(out=w3_c[:].bitcast(E4M3), scales=w3_sc[:], in_=w3_bf[:])
         b_c = keep.tile([P, C], U32, name="b_c", align_bytes=64)
         b_sc = keep.tile([P, C], U8, name="b_sc", align_bytes=64)
-        a3_bf, a3_c, a3_sc = {}, {}, {}
 
-        def weave_a3(u):
-            a3_bf[u] = keep.tile([P, P * PACK], BF16, name=f"a3_bf{u}", align_bytes=64)
-            nc.scalar.copy(
-                a3_bf[u][:].rearrange("p (c i t) -> p c t i", i=4, t=PACK),
-                a34[u][:].rearrange("p t (c i) -> p c t i", i=4),
-            )
+        def pair_products(u, a34):
+            cols = slice(u * P, (u + 1) * P)
+            for t in range(PACK):
+                nc.vector.tensor_tensor(a34[:, t, :], a2[t][:].indirect(entries(p6, u * P, P)), b4[:, t, cols], ALU.mult)
+            woven = keep.tile([P, P * PACK], BF16, name=f"a3_bf{u}", align_bytes=64)
+            interleave(woven, a34)
+            return woven
 
-        def quantise_a3(u):
-            a3_c[u] = keep.tile([P, P], U32, name=f"a3_c{u}", align_bytes=64)
-            a3_sc[u] = keep.tile([P, P], U8, name=f"a3_sc{u}", align_bytes=64)
-            nc.vector.quantize_mx(out=a3_c[u][:].bitcast(E4M3), scales=a3_sc[u][:], in_=a3_bf[u][:])
+        def out_rows(g, i):
+            return slice((2 * g + i) * P, (2 * g + i + 1) * P)
 
-        ys, juries, turns, wholes, fracs = {}, {}, {}, {}, {}
+        banks = [(u, g) for u in range(HALVES) for g in range(PAIRS)]
+        a3_bf = [pair_products(0, keep.tile([P, PACK, P], F32, name="a34_0"))]
+        nc.vector.quantize_mx(out=b_c[:].bitcast(E4M3), scales=b_sc[:], in_=b_bf[:])
 
-        def open_y(u, g):
-            ys[u, g] = psum.tile([P, 2, P], F32, name=f"y{u}{g}", tag=f"mark{2 * u + g}")
+        ys = {}
+        for u, g in banks:
+            ys[u, g] = psum.tile([P, 2, P], F32, name=f"y{u}{g}", tag=f"mark{PAIRS * u + g}")
             for i in range(2):
-                cols = slice((2 * g + i) * P, (2 * g + i + 1) * P)
                 nc.tensor.matmul_mx(
-                    out=ys[u, g][:, i, :], lhsT=w4_c[:, cols].bitcast(E4M3), lhsT_scale=w4_sc[:, 0, cols],
+                    out=ys[u, g][:, i, :], lhsT=w4_c[:, out_rows(g, i)].bitcast(E4M3), lhsT_scale=w4_sc[:, 0, out_rows(g, i)],
                     rhs=b_c[:, u * P : (u + 1) * P].bitcast(E4M3), rhs_scale=b_sc[:, u * P : (u + 1) * P],
                     start=(i == 0), stop=False,
                 )
-
-        def close_y(u, g):
+        a3_bf.append(pair_products(1, keep.tile([P, PACK, P], F32, name="a34_1", tag="b_bf", align_bytes=64)))
+        a3_c, a3_sc = [], []
+        for u in range(HALVES):
+            a3_c.append(keep.tile([P, P], U32, name=f"a3_c{u}", align_bytes=64))
+            a3_sc.append(keep.tile([P, P], U8, name=f"a3_sc{u}", align_bytes=64))
+            nc.vector.quantize_mx(out=a3_c[u][:].bitcast(E4M3), scales=a3_sc[u][:], in_=a3_bf[u][:])
+            for g in range(PAIRS):
+                for i in range(2):
+                    nc.tensor.matmul_mx(
+                        out=ys[u, g][:, i, :], lhsT=w3_c[:, out_rows(g, i)].bitcast(E4M3), lhsT_scale=w3_sc[:, out_rows(g, i)],
+                        rhs=a3_c[u][:].bitcast(E4M3), rhs_scale=a3_sc[u][:], start=False, stop=(i == 1),
+                    )
+        juries = {}
+        for u, g in banks:
+            juries[u, g] = psum.tile([P, 2, P], F32, name=f"jury{u}{g}", tag=f"bend{PAIRS * u + g}")
             for i in range(2):
-                cols = slice((2 * g + i) * P, (2 * g + i + 1) * P)
+                rows = out_rows(g, i)
                 nc.tensor.matmul_mx(
-                    out=ys[u, g][:, i, :], lhsT=w3_c[:, cols].bitcast(E4M3), lhsT_scale=w3_sc[:, cols],
-                    rhs=a3_c[u][:].bitcast(E4M3), rhs_scale=a3_sc[u][:], start=False, stop=(i == 1),
-                )
-
-        def jury_product(u, g):
-            juries[u, g] = psum.tile([P, 2, P], F32, name=f"jury{u}{g}", tag=f"bend{2 * u + g}")
-            for i in range(2):
-                m = 2 * g + i
-                nc.tensor.matmul_mx(
-                    out=juries[u, g][:, i, :], lhsT=w5_c[:, 2 * m * P : 2 * (m + 1) * P].bitcast(E2M1),
-                    lhsT_scale=w5_sc[:, 0, m * P : (m + 1) * P],
+                    out=juries[u, g][:, i, :],
+                    lhsT=w5_c[:, 2 * rows.start : 2 * rows.stop].bitcast(E2M1),
+                    lhsT_scale=w5_sc[:, 0, rows],
                     rhs=a3_c[u][:].bitcast(E4M3), rhs_scale=a3_sc[u][:], start=True, stop=True,
                 )
 
-        def reduce_angle(u):
-            for g in range(2):
-                turns[g] = ring.tile([P, 2, P], F32, name="turn", tag="th")
+        fracs = {}
+        for u in range(HALVES):
+            turns, wholes = [], []
+            for g in range(PAIRS):
+                turns.append(ring.tile([P, 2, P], F32, name="turn", tag="tanh"))
                 nc.scalar.activation(turns[g][:], ys[u, g][:], ACT.Copy, scale=1.0 / (2.0 * math.pi))
-            for g in range(2):
-                wholes[g] = ring.tile([P, 2, P], I32, name="whole", tag="mk")
+            for g in range(PAIRS):
+                wholes.append(ring.tile([P, 2, P], I32, name="whole", tag="mark_sb"))
                 nc.vector.tensor_scalar(wholes[g][:], turns[g][:], ROUNDER, ROUNDER, ALU.add, ALU.subtract)
-            for g in range(2):
+            for g in range(PAIRS):
                 fracs[u, g] = ring.tile([P, 2, P], F32, name="frac", tag="left")
                 nc.vector.tensor_tensor(fracs[u, g][:], turns[g][:], wholes[g][:], ALU.subtract)
-
-        def finish(u):
-            for g in range(2):
-                sine = ring.tile([P, 2, P], F32, name="sine", tag="right")
-                nc.scalar.activation(sine[:], fracs[u, g][:], ACT.Sin, scale=2.0 * math.pi)
-                score = ring.tile([P, 2, P], F32, name="score")
-                nc.vector.tensor_tensor(score[:], juries[u, g][:], sine[:], ALU.mult)
-                rows = out[2 * g * P : 2 * (g + 1) * P, u * P : (u + 1) * P]
-                nc.sync.dma_start(rows.rearrange("(i p) c -> p i c", i=2), score[:])
-
-        a34[0] = keep.tile([P, PACK, P], F32, name="a34_0")
-        for t in range(PACK):
-            competitors_product(t, 0)
-        weave_a3(0)
-        nc.vector.quantize_mx(out=b_c[:].bitcast(E4M3), scales=b_sc[:], in_=b_bf[:])
-        for u in range(2):
-            for g in range(2):
-                open_y(u, g)
-        a34[1] = keep.tile([P, PACK, P], F32, name="a34_1", tag="b_bf", align_bytes=64)
-        for t in range(PACK):
-            competitors_product(t, 1)
-        weave_a3(1)
-        for u in range(2):
-            quantise_a3(u)
-            for g in range(2):
-                close_y(u, g)
-        for u in range(2):
-            for g in range(2):
-                jury_product(u, g)
-        for u in range(2):
-            reduce_angle(u)
-        for u in range(2):
-            finish(u)
+        for u, g in banks:
+            sine = ring.tile([P, 2, P], F32, name="sine", tag="right")
+            nc.scalar.activation(sine[:], fracs[u, g][:], ACT.Sin, scale=2.0 * math.pi)
+            score = ring.tile([P, 2, P], F32, name="score")
+            nc.vector.tensor_tensor(score[:], juries[u, g][:], sine[:], ALU.mult)
+            block = out[2 * g * P : 2 * (g + 1) * P, u * P : (u + 1) * P]
+            nc.sync.dma_start(block.rearrange("(i p) c -> p i c", i=2), score[:])

import math
from contextlib import ExitStack

import concourse.mybir as mybir

K, H, N, T, S, A, B, C = 1024, 512, 512, 4096, 2048, 1024, 512, 256
FLOPS = 2 * (2 * K * H * S + 3 * H * N * C)

F32 = mybir.dt.float32
BF16 = mybir.dt.bfloat16
I32 = mybir.dt.int32
U32 = mybir.dt.uint32
U16 = mybir.dt.uint16
U8 = mybir.dt.uint8
E4M3 = mybir.dt.float8_e4m3fn_x4
E2M1 = mybir.dt.float4_e2m1fn_x4
ALU = mybir.AluOpType
ACT = mybir.ActivationFunctionType

P = 128
PACK = 4
LAST = PACK - 1
K_PASS = P * PACK
PASSES = K // K_PASS
QUADRANTS = 4
SCALE_ROWS = 16
TABLE_SCALES_AT = P - PASSES * SCALE_ROWS
CHUNK = 512
CHUNKS = S // CHUNK
LIST_ROWS = 16
RUN = 4
HALVES = C // P
PAIRS = N // (2 * P)
VECTOR_GATES = 5
ROUNDER = 1.5 * 2.0**23


def tile_list_bricklaying_jury_scores_kernel(
    tc, tab_words, tab_scales, w1, w2_words, w2_scales, w3, w4_words, w4_scales,
    w5_words, w5_scales, offs, pos1, pos2, pos3, pos4, pos5, pos6, out,
):
    nc = tc.nc
    with ExitStack() as ctx:
        lists = ctx.enter_context(tc.tile_pool(name="lists", bufs=1))
        keep = ctx.enter_context(tc.tile_pool(name="keep", bufs=1))
        ring = ctx.enter_context(tc.tile_pool(name="ring", bufs=4))
        psum = ctx.enter_context(tc.psum_pool(name="psum", bufs=1))

        def load_list(name, src):
            offsets = lists.tile([P, src.shape[1]], U16, name=name)
            nc.sync.dma_start(offsets[:], src)
            return offsets

        def entries(offsets, first, count):
            return offsets[:, first // LIST_ROWS : (first + count) // LIST_ROWS]

        def load_scale_rows(queue, scales, src):
            for q in range(QUADRANTS):
                queue.dma_start(
                    scales[32 * q : 32 * q + 4].bitcast(I32),
                    src[:, 4 * q : 4 * q + 4, :].rearrange("a s n -> s a n").bitcast(I32),
                )

        def load_table(a, tag):
            words = keep.tile([P, T], U32, name=f"tab_w{a}", tag=tag, align_bytes=64)
            nc.sync.dma_start(words[:].bitcast(I32), tab_words[a].rearrange("p t i -> p (t i)").bitcast(I32))
            return words

        def load_rows(name, src, tag):
            raw = keep.tile([P, PACK, src.shape[1]], F32, name=name, tag=tag, align_bytes=64)
            nc.sync.dma_start(raw[:], src.rearrange("(p j) n -> p j n", j=PACK))
            return raw

        def interleave(woven, rows):
            nc.scalar.copy(
                woven[:].rearrange("p (c i j) -> p c j i", i=RUN, j=PACK),
                rows[:].rearrange("p j (c i) -> p c j i", i=RUN),
            )

        idx = load_list("idx", offs)
        tab_sc = keep.tile([P, T], U8, name="tab_sc", tag="tab_sc", align_bytes=64)
        nc.sync.dma_start(tab_sc[TABLE_SCALES_AT:P, :].bitcast(I32), tab_scales.rearrange("a q t -> (a q) t").bitcast(I32))
        nc.vector.memset(tab_sc[0:TABLE_SCALES_AT, :].bitcast(I32), 0)
        w2_sc_raw = keep.tile([P, PASSES, H], U8, name="w2_sc_raw", align_bytes=64)
        nc.gpsimd.memset(w2_sc_raw[:].rearrange("p a n -> p (a n)").bitcast(I32), 0)
        load_scale_rows(nc.gpsimd, w2_sc_raw, w2_scales)
        v_sc = keep.tile([P, PASSES, S], U8, name="v_sc", align_bytes=64)
        nc.vector.memset(v_sc[:].rearrange("p a n -> p (a n)").bitcast(I32), 0)

        warm_in = keep.tile([P, 8], F32, name="warm_in")
        warm_out = keep.tile([P, 8], F32, name="warm_out")
        nc.gpsimd.memset(warm_in[:], 0.0)
        nc.scalar.activation(warm_out[:], warm_in[:], ACT.Silu)

        tab_w0 = load_table(0, "tab_w0")
        p1 = load_list("p1", pos1)
        p2 = load_list("p2", pos2)
        p3 = load_list("p3", pos3)
        p4 = load_list("p4", pos4)
        p5 = load_list("p5", pos5)
        p6 = load_list("p6", pos6)
        w1_raw = [load_rows("w1_raw0", w1[0:K_PASS, :], "raw0")]
        w2_raw = keep.tile([P, PASSES, 2 * H], U8, name="w2_raw", tag="w2_raw", align_bytes=64)
        nc.sync.dma_start(w2_raw[:].bitcast(I32), w2_words.rearrange("a p b -> p a b").bitcast(I32))
        w1_raw.append(load_rows("w1_raw1", w1[K_PASS:K, :], "raw1"))

        picked_sc = keep.tile([P, S], U8, name="picked_sc", align_bytes=64)
        nc.vector.tensor_copy(picked_sc[:], tab_sc[:].indirect(idx[:]))
        for a, queue in enumerate((nc.sync, nc.gpsimd)):
            for q in range(QUADRANTS):
                row = TABLE_SCALES_AT + SCALE_ROWS * a + 4 * q
                queue.dma_start(v_sc[32 * q : 32 * q + 4, a, :].bitcast(I32), picked_sc[row : row + 4, :].bitcast(I32))

        tab_w1 = load_table(1, "tab_sc")
        v0 = keep.tile([P, S], U32, name="v0", align_bytes=64)
        nc.vector.tensor_copy(v0[:], tab_w0[:].indirect(idx[:]))

        w2_c = keep.tile([P, PASSES, PACK, 2 * P], U8, name="w2_c", tag="tab_w0", align_bytes=64)
        nc.vector.tensor_copy(w2_c[:].bitcast(U16), w2_raw[:].bitcast(U16).rearrange("p a (m t) -> p a t m", t=PACK))
        w2_sc = keep.tile([P, PASSES, PACK, P], U8, name="w2_sc", tag="w2_raw", align_bytes=64)
        nc.vector.tensor_copy(w2_sc[:], w2_sc_raw[:].rearrange("p a (m t) -> p a t m", t=PACK))

        w1_c = [keep.tile([P, H], U32, name=f"w1_c{a}", align_bytes=64) for a in range(PASSES)]
        w1_sc = [keep.tile([P, H], U8, name=f"w1_sc{a}", align_bytes=64) for a in range(PASSES)]
        for a in range(PASSES):
            w1_bf = keep.tile([P, H * PACK], BF16, name=f"w1_bf{a}", tag=f"w1_bf{a}", align_bytes=64)
            nc.scalar.copy(
                w1_bf[:].rearrange("p (t m j) -> p m t j", t=PACK, j=PACK),
                w1_raw[a][:].rearrange("p j (m t) -> p m t j", t=PACK),
            )
            nc.vector.quantize_mx(out=w1_c[a][:].bitcast(E4M3), scales=w1_sc[a][:], in_=w1_bf[:])

        v1 = []
        for c in range(CHUNKS):
            words = keep.tile([P, CHUNK], U32, name=f"v1_{c}", align_bytes=64)
            nc.vector.tensor_copy(words[:], tab_w1[:].indirect(entries(idx, c * CHUNK, CHUNK)))
            v1.append(words)

        w3_raw = load_rows("w3_raw", w3, "raw1")
        w4_c = keep.tile([P, N], U32, name="w4_c", tag="w1_bf0", align_bytes=64)
        nc.sync.dma_start(w4_c[:].bitcast(I32), w4_words[0].rearrange("p n i -> p (n i)").bitcast(I32))
        w45_sc = keep.tile([P, 2, N], U8, name="w45_sc", tag="tab_sc", align_bytes=64)
        nc.gpsimd.memset(w45_sc[:].rearrange("p w n -> p (w n)").bitcast(I32), 0)
        w4_sc, w5_sc = w45_sc[:, 0:1, :], w45_sc[:, 1:2, :]
        load_scale_rows(nc.sync, w4_sc, w4_scales)
        load_scale_rows(nc.sync, w5_sc, w5_scales)

        def table_pass(bank, codes, scales, c, a):
            cols = slice(c * CHUNK, (c + 1) * CHUNK)
            words = v0[:, cols] if a == 0 else v1[c][:]
            nc.tensor.matmul_mx(
                out=bank[:], lhsT=codes, lhsT_scale=scales, rhs=words.bitcast(E4M3), rhs_scale=v_sc[:, a, cols],
                start=(a == 0), stop=(a == PASSES - 1),
            )

        tanh_heir = {(LAST, CHUNKS - 1): "a1_1", divmod(VECTOR_GATES - 1, CHUNKS): "second0"}
        mark_heir = {(LAST, CHUNKS - 1): "a1_0", (LAST, 1): "w3_bf"}

        def chunk_tile(name, heir):
            if heir is None:
                return ring.tile([P, CHUNK], F32, name=name, tag=name)
            return keep.tile([P, CHUNK], F32, name=f"{name}_{heir}", tag=heir, align_bytes=64)

        h = [keep.tile([P, S], F32, name=f"h{t}") for t in range(PACK)]
        b4 = keep.tile([P, PACK, C], F32, name="b4")
        for t in range(PACK):
            marks = [psum.tile([P, CHUNK], F32, name=f"mark{c}", tag=f"mark{c}") for c in range(CHUNKS)]
            bends = [psum.tile([P, CHUNK], F32, name=f"bend{c}", tag=f"bend{c}") for c in range(CHUNKS)]
            if t == 0:
                order = [(c, a) for a in range(PASSES) for c in range(CHUNKS)]
            else:
                order = [(c, a) for c in range(CHUNKS) for a in range(PASSES)]
            dealt = slice(t * P, (t + 1) * P)
            for c, a in order:
                table_pass(bends[c], w2_c[:, a, t, :].bitcast(E2M1), w2_sc[:, a, t, :], c, a)
                table_pass(marks[c], w1_c[a][:, dealt].bitcast(E4M3), w1_sc[a][:, dealt], c, a)
                if a == PASSES - 1:
                    gated = h[t][:, c * CHUNK : (c + 1) * CHUNK]
                    tanh = chunk_tile("tanh", tanh_heir.get((t, c)))
                    nc.scalar.activation(tanh[:], bends[c][:], ACT.Tanh)
                    if t * CHUNKS + c < VECTOR_GATES:
                        nc.vector.tensor_tensor(gated, marks[c][:], tanh[:], ALU.mult)
                    else:
                        mark_sb = chunk_tile("mark_sb", mark_heir.get((t, c)))
                        nc.scalar.copy(mark_sb[:], marks[c][:])
                        nc.gpsimd.tensor_tensor(gated, mark_sb[:], tanh[:], ALU.mult)

        w3_bf = keep.tile([P, N * PACK], BF16, name="w3_bf", tag="w3_bf", align_bytes=64)
        interleave(w3_bf, w3_raw)
        w5_c = keep.tile([P, 2 * N], U8, name="w5_c", tag="raw1", align_bytes=64)
        nc.sync.dma_start(w5_c[:].bitcast(I32), w5_words[0].bitcast(I32))

        courses = []
        for t in range(PACK):
            first = keep.tile([P, A], F32, name=f"first{t}", tag=f"first{t}", align_bytes=64)
            second = keep.tile([P, A], F32, name=f"second{t}", tag=f"second{t}", align_bytes=64)
            nc.vector.tensor_copy(first[:], h[t][:].indirect(p1[:]))
            nc.vector.tensor_copy(second[:], h[t][:].indirect(p2[:]))
            courses.append((first, second))
        a1 = []
        for t, tag in enumerate(("a1_0", "a1_1", "first0", "a1_3")):
            a1.append(keep.tile([P, A], F32, name=f"a1_{t}", tag=tag, align_bytes=64))
            nc.gpsimd.tensor_tensor(a1[t][:], courses[t][0][:], courses[t][1][:], ALU.add)

        walls = []
        for t in range(PACK):
            left = ring.tile([P, B], F32, name="left", tag="left")
            right = ring.tile([P, B], F32, name="right", tag="right")
            nc.vector.tensor_copy(left[:], a1[t][:].indirect(p3[:]))
            nc.vector.tensor_copy(right[:], a1[t][:].indirect(p4[:]))
            walls.append((left, right))
        a2 = []
        for t, tag in enumerate((f"first{LAST}", f"second{LAST}", "a2_2", "a2_3")):
            a2.append(keep.tile([P, B], F32, name=f"a2_{t}", tag=tag, align_bytes=64))
            nc.vector.tensor_tensor(a2[t][:], walls[t][0][:], walls[t][1][:], ALU.max)

        for t in range(PACK):
            nc.vector.tensor_copy(b4[:, t, :], a2[t][:].indirect(p5[:]))
        b_bf = keep.tile([P, C * PACK], BF16, name="b_bf", tag="b_bf", align_bytes=64)
        interleave(b_bf, b4)
        w3_c = keep.tile([P, N], U32, name="w3_c", tag="a1_3", align_bytes=64)
        w3_sc = keep.tile([P, N], U8, name="w3_sc", align_bytes=64)
        nc.vector.quantize_mx(out=w3_c[:].bitcast(E4M3), scales=w3_sc[:], in_=w3_bf[:])
        b_c = keep.tile([P, C], U32, name="b_c", align_bytes=64)
        b_sc = keep.tile([P, C], U8, name="b_sc", align_bytes=64)

        def pair_products(u, a34):
            cols = slice(u * P, (u + 1) * P)
            for t in range(PACK):
                nc.vector.tensor_tensor(a34[:, t, :], a2[t][:].indirect(entries(p6, u * P, P)), b4[:, t, cols], ALU.mult)
            woven = keep.tile([P, P * PACK], BF16, name=f"a3_bf{u}", align_bytes=64)
            interleave(woven, a34)
            return woven

        def out_rows(g, i):
            return slice((2 * g + i) * P, (2 * g + i + 1) * P)

        banks = [(u, g) for u in range(HALVES) for g in range(PAIRS)]
        a3_bf = [pair_products(0, keep.tile([P, PACK, P], F32, name="a34_0"))]
        nc.vector.quantize_mx(out=b_c[:].bitcast(E4M3), scales=b_sc[:], in_=b_bf[:])

        ys = {}
        for u, g in banks:
            ys[u, g] = psum.tile([P, 2, P], F32, name=f"y{u}{g}", tag=f"mark{PAIRS * u + g}")
            for i in range(2):
                nc.tensor.matmul_mx(
                    out=ys[u, g][:, i, :], lhsT=w4_c[:, out_rows(g, i)].bitcast(E4M3), lhsT_scale=w4_sc[:, 0, out_rows(g, i)],
                    rhs=b_c[:, u * P : (u + 1) * P].bitcast(E4M3), rhs_scale=b_sc[:, u * P : (u + 1) * P],
                    start=(i == 0), stop=False,
                )
        a3_bf.append(pair_products(1, keep.tile([P, PACK, P], F32, name="a34_1", tag="b_bf", align_bytes=64)))
        a3_c, a3_sc = [], []
        for u in range(HALVES):
            a3_c.append(keep.tile([P, P], U32, name=f"a3_c{u}", align_bytes=64))
            a3_sc.append(keep.tile([P, P], U8, name=f"a3_sc{u}", align_bytes=64))
            nc.vector.quantize_mx(out=a3_c[u][:].bitcast(E4M3), scales=a3_sc[u][:], in_=a3_bf[u][:])
            for g in range(PAIRS):
                for i in range(2):
                    nc.tensor.matmul_mx(
                        out=ys[u, g][:, i, :], lhsT=w3_c[:, out_rows(g, i)].bitcast(E4M3), lhsT_scale=w3_sc[:, out_rows(g, i)],
                        rhs=a3_c[u][:].bitcast(E4M3), rhs_scale=a3_sc[u][:], start=False, stop=(i == 1),
                    )
        juries = {}
        for u, g in banks:
            juries[u, g] = psum.tile([P, 2, P], F32, name=f"jury{u}{g}", tag=f"bend{PAIRS * u + g}")
            for i in range(2):
                rows = out_rows(g, i)
                nc.tensor.matmul_mx(
                    out=juries[u, g][:, i, :],
                    lhsT=w5_c[:, 2 * rows.start : 2 * rows.stop].bitcast(E2M1),
                    lhsT_scale=w5_sc[:, 0, rows],
                    rhs=a3_c[u][:].bitcast(E4M3), rhs_scale=a3_sc[u][:], start=True, stop=True,
                )

        fracs = {}
        for u in range(HALVES):
            turns, wholes = [], []
            for g in range(PAIRS):
                turns.append(ring.tile([P, 2, P], F32, name="turn", tag="tanh"))
                nc.scalar.activation(turns[g][:], ys[u, g][:], ACT.Copy, scale=1.0 / (2.0 * math.pi))
            for g in range(PAIRS):
                wholes.append(ring.tile([P, 2, P], I32, name="whole", tag="mark_sb"))
                nc.vector.tensor_scalar(wholes[g][:], turns[g][:], ROUNDER, ROUNDER, ALU.add, ALU.subtract)
            for g in range(PAIRS):
                fracs[u, g] = ring.tile([P, 2, P], F32, name="frac", tag="left")
                nc.vector.tensor_tensor(fracs[u, g][:], turns[g][:], wholes[g][:], ALU.subtract)
        for u, g in banks:
            sine = ring.tile([P, 2, P], F32, name="sine", tag="right")
            nc.scalar.activation(sine[:], fracs[u, g][:], ACT.Sin, scale=2.0 * math.pi)
            score = ring.tile([P, 2, P], F32, name="score")
            nc.vector.tensor_tensor(score[:], juries[u, g][:], sine[:], ALU.mult)
            block = out[2 * g * P : 2 * (g + 1) * P, u * P : (u + 1) * P]
            nc.sync.dma_start(block.rearrange("(i p) c -> p i c", i=2), score[:])
